import numpy as np
import ml_dtypes


def mxq(x, axis, fmt="e4m3"):
    dtype, down = {"e4m3": (ml_dtypes.float8_e4m3fn, 7), "e5m2": (ml_dtypes.float8_e5m2, 14)}[fmt]
    v = np.moveaxis(np.asarray(x, np.float32).astype(ml_dtypes.bfloat16).astype(np.float64), axis, -1)
    blocks = v.reshape(v.shape[:-1] + (-1, 32))
    amax = np.abs(blocks).max(-1, keepdims=True)
    byte = np.maximum(np.where(amax > 0, np.frexp(amax)[1] - 1 + 127, 0) - down, 1)
    scale = np.exp2(byte - 127.0)
    codes = (blocks / scale).astype(np.float32).astype(dtype).astype(np.float64)
    return np.moveaxis((codes * scale).reshape(v.shape), -1, axis)


WIDE = False


def mx_kscale(k):
    if not WIDE:
        return np.ones(k)
    levels = np.array([18, -18])
    if k % 512:
        return np.exp2(np.random.permutation(np.resize(levels, k // 32))).repeat(32)
    a = np.empty((k // 512, 16))
    for p in range(k // 512):
        a[p, :8] = np.random.permutation(np.resize(levels, 8))
        for g in range(8):
            far = levels[np.abs(levels - a[p, g]) >= 10]
            a[p, g + 8] = far[np.random.randint(len(far))]
    return np.exp2(a.ravel()).repeat(32)


def f64(x):
    return np.asarray(x).astype(np.float64)


def striped(idx):
    return np.tile(np.asarray(idx).reshape(-1, 16).T, (8, 1)).astype(np.uint16)


def unstriped(offs):
    return offs[:16].T.reshape(-1).astype(np.int64)


def setup_inputs():
    n = np.random.standard_normal
    uni = np.random.uniform
    idx = np.random.permutation(2048)[:512]
    f_d = mx_kscale(512)
    return {
        "dyT": (n((512, 2048)) * f_d[:, None]).astype(np.float32),
        "oT": (n((512, 2048))).astype(np.float32),
        "wo": (n((512, 512)) / np.sqrt(512) / f_d[:, None]).astype(np.float32),
        "gq": np.tile(uni(0.75, 1.3, 2048), (128, 1)).astype(np.float32),
        "offs": striped(idx),
    }


def reference(dyT, oT, wo, gq, offs):
    idx = unstriped(offs)
    dyT_i = f64(dyT)[:, idx]
    o_ = f64(oT)[:, idx]
    gq_i = f64(gq)[:1][:, idx]
    b = mxq(f64(wo), 0, "e4m3").T @ mxq(dyT_i, 0, "e5m2")
    do = gq_i * b
    q = do * o_
    qt = q.T
    dl = (qt).sum(-1, keepdims=True)
    out_0 = np.zeros((512, 2048))
    out_0[:, idx] = do
    out_1 = dl.T
    return out_0, out_1

@@ -1,0 +1,161 @@
+from contextlib import ExitStack
+
+import concourse.mybir as mybir
+from concourse.masks import make_identity
+
+D, E, T, N = 512, 512, 2048, 512
+FLOPS = 2 * D * E * N
+BYTES = 4 * (D * T + E * T + D * E + T + E * T + N) + 2 * 128 * (N // 16)
+
+F32 = mybir.dt.float32
+BF16 = mybir.dt.bfloat16
+U32 = mybir.dt.uint32
+U16 = mybir.dt.uint16
+U8 = mybir.dt.uint8
+E4M3 = mybir.dt.float8_e4m3fn_x4
+E5M2 = mybir.dt.float8_e5m2_x4
+MULT = mybir.AluOpType.mult
+COPY = mybir.ActivationFunctionType.Copy
+
+P = 128
+PACK = 4
+TILES = E // P
+BLOCKS = N // P
+WINDOWS = 3
+RUN = T // P
+
+
+def tile_attend_gdelta_kernel(tc, dyT, oT, wo, gq, offs, out_0, out_1):
+    nc = tc.nc
+    with ExitStack() as ctx:
+        keep = ctx.enter_context(tc.tile_pool(name="keep", bufs=1))
+        psum = ctx.enter_context(tc.psum_pool(name="psum", bufs=1))
+        psum_b = ctx.enter_context(tc.psum_pool(name="psum_b", bufs=2))
+
+        offsets = keep.tile([P, N // 16], U16, name="offsets")
+        dy_planes = [keep.tile([P, T], F32, name=f"dy{t}") for t in range(PACK)]
+        o_tiles = [keep.tile([P, T], F32, name=f"o{j}") for j in range(TILES)]
+        wo_parts = [(0, 128), (128, 256), (256, 512)]
+        wo_raw = [keep.tile([P, PACK, hi - lo], F32, name=f"wo_raw{lo}") for lo, hi in wo_parts]
+        dy_rows = dyT.rearrange("(p t) n -> t p n", t=PACK)
+
+        def load_wo(k):
+            lo, hi = wo_parts[k]
+            nc.sync.dma_start(wo_raw[k][:], wo[:, lo:hi].rearrange("(p t) c -> p t c", t=PACK))
+
+        def load_o(j):
+            nc.sync.dma_start(o_tiles[j][:], oT[j * P : (j + 1) * P, :])
+
+        gate_runs = keep.tile([P, RUN], F32, name="gate_runs")
+        nc.scalar.dma_start(gate_runs[:], gq[0:1, :].rearrange("o (p u) -> (o p) u", u=RUN))
+        nc.sync.dma_start(dy_planes[0][:], dy_rows[0])
+        nc.sync.dma_start(offsets[:], offs)
+        for t in range(1, PACK):
+            nc.sync.dma_start(dy_planes[t][:], dy_rows[t])
+        load_wo(0)
+        load_wo(1)
+        load_wo(2)
+        for j in range(TILES):
+            load_o(j)
+
+        windows = [keep.tile([P, T], F32, name=f"window{w}") for w in range(WINDOWS)]
+        for w in range(WINDOWS):
+            nc.vector.memset(windows[w][:], 0.0)
+        identity = keep.tile([P, P], F32, name="identity")
+        make_identity(nc, identity[:])
+        delta_cols = keep.tile([P, P], F32, name="delta_cols")
+        nc.gpsimd.memset(delta_cols[:], 0.0)
+
+        dy_words = keep.tile([P, N, PACK], BF16, name="dy_words", align_bytes=64)
+
+        def gather_dy(t):
+            nc.vector.tensor_copy(dy_words[:, :, t], dy_planes[t][:].indirect(offsets[:]))
+
+        gate_window = keep.tile([P, T], F32, name="gate_window")
+        for a in range(RUN // BLOCKS):
+            spread = psum.tile([P, BLOCKS, P], F32, name=f"spread{a}", tag=f"bank{a}")
+            for u in range(BLOCKS):
+                column = a * BLOCKS + u
+                nc.tensor.transpose(
+                    spread[:, u, :], gate_runs[:, column : column + 1].to_broadcast([P, P]), identity[:]
+                )
+            nc.scalar.activation(
+                gate_window[:].rearrange("p (k u) -> p k u", u=RUN)[:, :, a * BLOCKS : (a + 1) * BLOCKS],
+                spread[:].rearrange("p u k -> p k u"),
+                COPY,
+            )
+
+        gather_dy(0)
+        gather_dy(1)
+        gate = keep.tile([P, N], F32, name="gate")
+        nc.vector.tensor_copy(gate[:], gate_window[:].indirect(offsets[:]))
+        gather_dy(2)
+        gather_dy(3)
+
+        turned = psum.tile([P, BLOCKS, P], F32, name="turned", tag="turned")
+        for c in range(BLOCKS):
+            nc.tensor.transpose(turned[:, c, :], gate[:, c * P : (c + 1) * P], identity[:])
+        gate_cols = keep.tile([P, BLOCKS], F32, name="gate_cols")
+        nc.scalar.copy(gate_cols[:], turned[:, :, 0])
+
+        dy_codes = keep.tile([P, N], U32, name="dy_codes", align_bytes=64)
+        dy_scales = keep.tile([P, N], U8, name="dy_scales", align_bytes=64)
+        nc.vector.quantize_mx(
+            out=dy_codes[:].bitcast(E5M2), scales=dy_scales[:], in_=dy_words[:].rearrange("p n t -> p (n t)")
+        )
+
+        stationary = []
+        for k, (lo, hi) in enumerate(wo_parts):
+            width = hi - lo
+            wo_words = keep.tile([P, width, PACK], BF16, name=f"wo_words{lo}", align_bytes=64)
+            nc.scalar.copy(
+                wo_words[:].rearrange("p (c i) t -> p c t i", i=4),
+                wo_raw[k][:].rearrange("p t (c i) -> p c t i", i=4),
+            )
+            wo_codes = keep.tile([P, width], U32, name=f"wo_codes{lo}", align_bytes=64)
+            wo_scales = keep.tile([P, width], U8, name=f"wo_scales{lo}", align_bytes=64)
+            nc.vector.quantize_mx(
+                out=wo_codes[:].bitcast(E4M3), scales=wo_scales[:], in_=wo_words[:].rearrange("p c t -> p (c t)")
+            )
+            for m in range(0, width, P):
+                stationary.append((wo_codes[:, m : m + P], wo_scales[:, m : m + P]))
+
+        sums = [psum.tile([P, P], F32, name=f"sums{c}", tag=f"bank{c}") for c in range(BLOCKS)]
+        for j in range(TILES):
+            bank = psum_b.tile([P, N], F32, name="bank")
+            nc.tensor.matmul_mx(
+                out=bank[:],
+                lhsT=stationary[j][0].bitcast(E4M3),
+                lhsT_scale=stationary[j][1],
+                rhs=dy_codes[:].bitcast(E5M2),
+                rhs_scale=dy_scales[:],
+                start=True,
+                stop=True,
+            )
+            b = keep.tile([P, N], F32, name=f"b{j}")
+            nc.scalar.copy(b[:], bank[:])
+            window = windows[j % WINDOWS]
+            nc.vector.tensor_tensor(window[:].indirect(offsets[:]), b[:], gate[:], MULT)
+            nc.sync.dma_start(out_0[j * P : (j + 1) * P, :], window[:])
+            q = keep.tile([P, N], F32, name=f"q{j}")
+            nc.vector.tensor_tensor(q[:], o_tiles[j][:].indirect(offsets[:]), b[:], MULT)
+            for c in range(BLOCKS):
+                nc.tensor.matmul(
+                    sums[c][:],
+                    q[:, c * P : (c + 1) * P],
+                    identity[:],
+                    start=(j == 0),
+                    stop=(j == TILES - 1),
+                    is_transpose=True,
+                )
+
+        gated = keep.tile([P, BLOCKS, P], F32, name="gated")
+        for c in range(BLOCKS):
+            nc.scalar.activation(
+                gated[:, c, :], sums[c][:], COPY, scale=gate_cols[:, c : c + 1], accum_out=delta_cols[:, c : c + 1]
+            )
+        delta_turned = psum.tile([P, P], F32, name="delta_turned", tag="turned")
+        nc.tensor.transpose(delta_turned[:], delta_cols[:], identity[:])
+        delta_rows = keep.tile([32, P], F32, name="delta_rows")
+        nc.scalar.copy(delta_rows[:], delta_turned[0:32, :])
+        nc.scalar.dma_start(out_1.rearrange("o (c p) -> (o c) p", p=P), delta_rows[0:BLOCKS, :])

@@ -35,12 +35,13 @@ def tile_attend_gdelta_kernel(tc, dyT, oT, wo, gq, offs, out_0, out_1):
         offsets = keep.tile([P, N // 16], U16, name="offsets")
         dy_planes = [keep.tile([P, T], F32, name=f"dy{t}") for t in range(PACK)]
         o_tiles = [keep.tile([P, T], F32, name=f"o{j}") for j in range(TILES)]
-        wo_parts = [(0, 128), (128, 256), (256, 512)]
-        wo_raw = [keep.tile([P, PACK, hi - lo], F32, name=f"wo_raw{lo}") for lo, hi in wo_parts]
+        wo_loads = [(0, 256), (256, 512)]
+        wo_parts = [(0, 0, 128), (0, 128, 256), (1, 0, 128), (1, 128, 256)]
+        wo_raw = [keep.tile([P, PACK, hi - lo], F32, name=f"wo_raw{lo}") for lo, hi in wo_loads]
         dy_rows = dyT.rearrange("(p t) n -> t p n", t=PACK)
 
         def load_wo(k):
-            lo, hi = wo_parts[k]
+            lo, hi = wo_loads[k]
             nc.sync.dma_start(wo_raw[k][:], wo[:, lo:hi].rearrange("(p t) c -> p t c", t=PACK))
 
         def load_o(j):
@@ -54,15 +55,15 @@ def tile_attend_gdelta_kernel(tc, dyT, oT, wo, gq, offs, out_0, out_1):
             nc.sync.dma_start(dy_planes[t][:], dy_rows[t])
         load_wo(0)
         load_wo(1)
-        load_wo(2)
         for j in range(TILES):
             load_o(j)
 
         windows = [keep.tile([P, T], F32, name=f"window{w}") for w in range(WINDOWS)]
-        for w in range(WINDOWS):
+        for w in range(WINDOWS - 1):
             nc.vector.memset(windows[w][:], 0.0)
         identity = keep.tile([P, P], F32, name="identity")
         make_identity(nc, identity[:])
+        nc.gpsimd.memset(windows[WINDOWS - 1][:], 0.0)
         delta_cols = keep.tile([P, P], F32, name="delta_cols")
         nc.gpsimd.memset(delta_cols[:], 0.0)
 
@@ -85,18 +86,8 @@ def tile_attend_gdelta_kernel(tc, dyT, oT, wo, gq, offs, out_0, out_1):
                 COPY,
             )
 
-        gather_dy(0)
-        gather_dy(1)
-        gate = keep.tile([P, N], F32, name="gate")
-        nc.vector.tensor_copy(gate[:], gate_window[:].indirect(offsets[:]))
-        gather_dy(2)
-        gather_dy(3)
-
-        turned = psum.tile([P, BLOCKS, P], F32, name="turned", tag="turned")
-        for c in range(BLOCKS):
-            nc.tensor.transpose(turned[:, c, :], gate[:, c * P : (c + 1) * P], identity[:])
-        gate_cols = keep.tile([P, BLOCKS], F32, name="gate_cols")
-        nc.scalar.copy(gate_cols[:], turned[:, :, 0])
+        for t in range(PACK):
+            gather_dy(t)
 
         dy_codes = keep.tile([P, N], U32, name="dy_codes", align_bytes=64)
         dy_scales = keep.tile([P, N], U8, name="dy_scales", align_bytes=64)
@@ -105,24 +96,41 @@ def tile_attend_gdelta_kernel(tc, dyT, oT, wo, gq, offs, out_0, out_1):
         )
 
         stationary = []
-        for k, (lo, hi) in enumerate(wo_parts):
+
+        def quantize_wo(k):
+            load, lo, hi = wo_parts[k]
             width = hi - lo
-            wo_words = keep.tile([P, width, PACK], BF16, name=f"wo_words{lo}", align_bytes=64)
+            wo_words = keep.tile([P, width, PACK], BF16, name=f"wo_words{k}", tag=("z", "w", "x", "y")[k], align_bytes=64)
             nc.scalar.copy(
                 wo_words[:].rearrange("p (c i) t -> p c t i", i=4),
-                wo_raw[k][:].rearrange("p t (c i) -> p c t i", i=4),
+                wo_raw[load][:, :, lo:hi].rearrange("p t (c i) -> p c t i", i=4),
             )
-            wo_codes = keep.tile([P, width], U32, name=f"wo_codes{lo}", align_bytes=64)
-            wo_scales = keep.tile([P, width], U8, name=f"wo_scales{lo}", align_bytes=64)
+            wo_codes = keep.tile([P, width], U32, name=f"wo_codes{k}", tag=("x", "y", "u", "v")[k], align_bytes=64)
+            wo_scales = keep.tile([P, width], U8, name=f"wo_scales{k}", align_bytes=64)
             nc.vector.quantize_mx(
                 out=wo_codes[:].bitcast(E4M3), scales=wo_scales[:], in_=wo_words[:].rearrange("p c t -> p (c t)")
             )
             for m in range(0, width, P):
                 stationary.append((wo_codes[:, m : m + P], wo_scales[:, m : m + P]))
 
+        quantize_wo(0)
+        gate = keep.tile([P, N], F32, name="gate", tag="z", align_bytes=64)
+        nc.vector.tensor_copy(gate[:], gate_window[:].indirect(offsets[:]))
+        quantize_wo(1)
+
+        gate_cols = keep.tile([P, BLOCKS], F32, name="gate_cols")
+
+        def turn_gates():
+            turned = psum_b.tile([P, BLOCKS, P], F32, name="turned", tag="ring")
+            for c in range(BLOCKS):
+                nc.tensor.transpose(turned[:, c, :], gate[:, c * P : (c + 1) * P], identity[:])
+            nc.scalar.copy(gate_cols[:], turned[:, :, 0])
+
         sums = [psum.tile([P, P], F32, name=f"sums{c}", tag=f"bank{c}") for c in range(BLOCKS)]
-        for j in range(TILES):
-            bank = psum_b.tile([P, N], F32, name="bank")
+        b = [keep.tile([P, N], F32, name=f"b{j}") for j in range(TILES)]
+
+        def product_and_scatter(j):
+            bank = psum_b.tile([P, N], F32, name="bank", tag="ring")
             nc.tensor.matmul_mx(
                 out=bank[:],
                 lhsT=stationary[j][0].bitcast(E4M3),
@@ -132,13 +140,14 @@ def tile_attend_gdelta_kernel(tc, dyT, oT, wo, gq, offs, out_0, out_1):
                 start=True,
                 stop=True,
             )
-            b = keep.tile([P, N], F32, name=f"b{j}")
-            nc.scalar.copy(b[:], bank[:])
+            nc.scalar.copy(b[j][:], bank[:])
             window = windows[j % WINDOWS]
-            nc.vector.tensor_tensor(window[:].indirect(offsets[:]), b[:], gate[:], MULT)
+            nc.vector.tensor_tensor(window[:].indirect(offsets[:]), b[j][:], gate[:], MULT)
             nc.sync.dma_start(out_0[j * P : (j + 1) * P, :], window[:])
-            q = keep.tile([P, N], F32, name=f"q{j}")
-            nc.vector.tensor_tensor(q[:], o_tiles[j][:].indirect(offsets[:]), b[:], MULT)
+
+        def add_to_delta(j):
+            q = keep.tile([P, N], F32, name=f"q{j}", tag=("x", "y", "q2", "q3")[j], align_bytes=64)
+            nc.vector.tensor_tensor(q[:], o_tiles[j][:].indirect(offsets[:]), b[j][:], MULT)
             for c in range(BLOCKS):
                 nc.tensor.matmul(
                     sums[c][:],
@@ -149,12 +158,23 @@ def tile_attend_gdelta_kernel(tc, dyT, oT, wo, gq, offs, out_0, out_1):
                     is_transpose=True,
                 )
 
+        product_and_scatter(0)
+        product_and_scatter(1)
+        quantize_wo(2)
+        quantize_wo(3)
+        turn_gates()
+        add_to_delta(0)
+        add_to_delta(1)
+        for j in (2, 3):
+            product_and_scatter(j)
+            add_to_delta(j)
+
         gated = keep.tile([P, BLOCKS, P], F32, name="gated")
         for c in range(BLOCKS):
             nc.scalar.activation(
                 gated[:, c, :], sums[c][:], COPY, scale=gate_cols[:, c : c + 1], accum_out=delta_cols[:, c : c + 1]
             )
-        delta_turned = psum.tile([P, P], F32, name="delta_turned", tag="turned")
+        delta_turned = psum_b.tile([P, P], F32, name="delta_turned", tag="ring")
         nc.tensor.transpose(delta_turned[:], delta_cols[:], identity[:])
         delta_rows = keep.tile([32, P], F32, name="delta_rows")
         nc.scalar.copy(delta_rows[:], delta_turned[0:32, :])

@@ -21,8 +21,15 @@ P = 128
 PACK = 4
 TILES = E // P
 BLOCKS = N // P
-WINDOWS = 3
 RUN = T // P
+LINE = 4
+QUADRANT = 32
+WINDOWS = 3
+WO_LOADS = [(0, 128), (128, 256), (256, 512)]
+WO_TILES = [(0, 0), (1, 0), (2, 0), (2, 128)]
+WORDS_TAGS = ("z", "w", "x", "y")
+CODES_TAGS = ("x", "y", "u", "v")
+TERMS_TAGS = ("x", "y", "q2", "q3")
 
 
 def tile_attend_gdelta_kernel(tc, dyT, oT, wo, gq, offs, out_0, out_1):
@@ -35,17 +42,8 @@ def tile_attend_gdelta_kernel(tc, dyT, oT, wo, gq, offs, out_0, out_1):
         offsets = keep.tile([P, N // 16], U16, name="offsets")
         dy_planes = [keep.tile([P, T], F32, name=f"dy{t}") for t in range(PACK)]
         o_tiles = [keep.tile([P, T], F32, name=f"o{j}") for j in range(TILES)]
-        wo_loads = [(0, 256), (256, 512)]
-        wo_parts = [(0, 0, 128), (0, 128, 256), (1, 0, 128), (1, 128, 256)]
-        wo_raw = [keep.tile([P, PACK, hi - lo], F32, name=f"wo_raw{lo}") for lo, hi in wo_loads]
+        wo_raw = [keep.tile([P, PACK, hi - lo], F32, name=f"wo_raw{lo}") for lo, hi in WO_LOADS]
         dy_rows = dyT.rearrange("(p t) n -> t p n", t=PACK)
-
-        def load_wo(k):
-            lo, hi = wo_loads[k]
-            nc.sync.dma_start(wo_raw[k][:], wo[:, lo:hi].rearrange("(p t) c -> p t c", t=PACK))
-
-        def load_o(j):
-            nc.sync.dma_start(o_tiles[j][:], oT[j * P : (j + 1) * P, :])
 
         gate_runs = keep.tile([P, RUN], F32, name="gate_runs")
         nc.scalar.dma_start(gate_runs[:], gq[0:1, :].rearrange("o (p u) -> (o p) u", u=RUN))
@@ -53,10 +51,10 @@ def tile_attend_gdelta_kernel(tc, dyT, oT, wo, gq, offs, out_0, out_1):
         nc.sync.dma_start(offsets[:], offs)
         for t in range(1, PACK):
             nc.sync.dma_start(dy_planes[t][:], dy_rows[t])
-        load_wo(0)
-        load_wo(1)
+        for raw, (lo, hi) in zip(wo_raw, WO_LOADS):
+            nc.sync.dma_start(raw[:], wo[:, lo:hi].rearrange("(p t) c -> p t c", t=PACK))
         for j in range(TILES):
-            load_o(j)
+            nc.sync.dma_start(o_tiles[j][:], oT[j * P : (j + 1) * P, :])
 
         windows = [keep.tile([P, T], F32, name=f"window{w}") for w in range(WINDOWS)]
         for w in range(WINDOWS - 1):
@@ -68,9 +66,6 @@ def tile_attend_gdelta_kernel(tc, dyT, oT, wo, gq, offs, out_0, out_1):
         nc.gpsimd.memset(delta_cols[:], 0.0)
 
         dy_words = keep.tile([P, N, PACK], BF16, name="dy_words", align_bytes=64)
-
-        def gather_dy(t):
-            nc.vector.tensor_copy(dy_words[:, :, t], dy_planes[t][:].indirect(offsets[:]))
 
         gate_window = keep.tile([P, T], F32, name="gate_window")
         for a in range(RUN // BLOCKS):
@@ -87,7 +82,7 @@ def tile_attend_gdelta_kernel(tc, dyT, oT, wo, gq, offs, out_0, out_1):
             )
 
         for t in range(PACK):
-            gather_dy(t)
+            nc.vector.tensor_copy(dy_words[:, :, t], dy_planes[t][:].indirect(offsets[:]))
 
         dy_codes = keep.tile([P, N], U32, name="dy_codes", align_bytes=64)
         dy_scales = keep.tile([P, N], U8, name="dy_scales", align_bytes=64)
@@ -97,21 +92,19 @@ def tile_attend_gdelta_kernel(tc, dyT, oT, wo, gq, offs, out_0, out_1):
 
         stationary = []
 
-        def quantize_wo(k):
-            load, lo, hi = wo_parts[k]
-            width = hi - lo
-            wo_words = keep.tile([P, width, PACK], BF16, name=f"wo_words{k}", tag=("z", "w", "x", "y")[k], align_bytes=64)
+        def quantize_wo(j):
+            load, lo = WO_TILES[j]
+            wo_words = keep.tile([P, P, PACK], BF16, name=f"wo_words{j}", tag=WORDS_TAGS[j], align_bytes=64)
             nc.scalar.copy(
-                wo_words[:].rearrange("p (c i) t -> p c t i", i=4),
-                wo_raw[load][:, :, lo:hi].rearrange("p t (c i) -> p c t i", i=4),
+                wo_words[:].rearrange("p (c i) t -> p c t i", i=LINE),
+                wo_raw[load][:, :, lo : lo + P].rearrange("p t (c i) -> p c t i", i=LINE),
             )
-            wo_codes = keep.tile([P, width], U32, name=f"wo_codes{k}", tag=("x", "y", "u", "v")[k], align_bytes=64)
-            wo_scales = keep.tile([P, width], U8, name=f"wo_scales{k}", align_bytes=64)
+            wo_codes = keep.tile([P, P], U32, name=f"wo_codes{j}", tag=CODES_TAGS[j], align_bytes=64)
+            wo_scales = keep.tile([P, P], U8, name=f"wo_scales{j}", align_bytes=64)
             nc.vector.quantize_mx(
                 out=wo_codes[:].bitcast(E4M3), scales=wo_scales[:], in_=wo_words[:].rearrange("p c t -> p (c t)")
             )
-            for m in range(0, width, P):
-                stationary.append((wo_codes[:, m : m + P], wo_scales[:, m : m + P]))
+            stationary.append((wo_codes, wo_scales))
 
         quantize_wo(0)
         gate = keep.tile([P, N], F32, name="gate", tag="z", align_bytes=64)
@@ -130,11 +123,12 @@ def tile_attend_gdelta_kernel(tc, dyT, oT, wo, gq, offs, out_0, out_1):
         b = [keep.tile([P, N], F32, name=f"b{j}") for j in range(TILES)]
 
         def product_and_scatter(j):
+            wo_codes, wo_scales = stationary[j]
             bank = psum_b.tile([P, N], F32, name="bank", tag="ring")
             nc.tensor.matmul_mx(
                 out=bank[:],
-                lhsT=stationary[j][0].bitcast(E4M3),
-                lhsT_scale=stationary[j][1],
+                lhsT=wo_codes[:].bitcast(E4M3),
+                lhsT_scale=wo_scales[:],
                 rhs=dy_codes[:].bitcast(E5M2),
                 rhs_scale=dy_scales[:],
                 start=True,
@@ -146,7 +140,7 @@ def tile_attend_gdelta_kernel(tc, dyT, oT, wo, gq, offs, out_0, out_1):
             nc.sync.dma_start(out_0[j * P : (j + 1) * P, :], window[:])
 
         def add_to_delta(j):
-            q = keep.tile([P, N], F32, name=f"q{j}", tag=("x", "y", "q2", "q3")[j], align_bytes=64)
+            q = keep.tile([P, N], F32, name=f"q{j}", tag=TERMS_TAGS[j], align_bytes=64)
             nc.vector.tensor_tensor(q[:], o_tiles[j][:].indirect(offsets[:]), b[j][:], MULT)
             for c in range(BLOCKS):
                 nc.tensor.matmul(
@@ -176,6 +170,6 @@ def tile_attend_gdelta_kernel(tc, dyT, oT, wo, gq, offs, out_0, out_1):
             )
         delta_turned = psum_b.tile([P, P], F32, name="delta_turned", tag="ring")
         nc.tensor.transpose(delta_turned[:], delta_cols[:], identity[:])
-        delta_rows = keep.tile([32, P], F32, name="delta_rows")
-        nc.scalar.copy(delta_rows[:], delta_turned[0:32, :])
+        delta_rows = keep.tile([QUADRANT, P], F32, name="delta_rows")
+        nc.scalar.copy(delta_rows[:], delta_turned[0:QUADRANT, :])
         nc.scalar.dma_start(out_1.rearrange("o (c p) -> (o c) p", p=P), delta_rows[0:BLOCKS, :])

@@ -56,12 +56,11 @@ def tile_attend_gdelta_kernel(tc, dyT, oT, wo, gq, offs, out_0, out_1):
         for j in range(TILES):
             nc.sync.dma_start(o_tiles[j][:], oT[j * P : (j + 1) * P, :])
 
-        windows = [keep.tile([P, T], F32, name=f"window{w}") for w in range(WINDOWS)]
-        for w in range(WINDOWS - 1):
-            nc.vector.memset(windows[w][:], 0.0)
+        windows = [keep.tile([P, T], F32, name=f"window{w}") for w in range(WINDOWS - 1)]
+        nc.vector.memset(windows[0][:], 0.0)
         identity = keep.tile([P, P], F32, name="identity")
         make_identity(nc, identity[:])
-        nc.gpsimd.memset(windows[WINDOWS - 1][:], 0.0)
+        nc.gpsimd.memset(windows[1][:], 0.0)
         delta_cols = keep.tile([P, P], F32, name="delta_cols")
         nc.gpsimd.memset(delta_cols[:], 0.0)
 
@@ -110,6 +109,9 @@ def tile_attend_gdelta_kernel(tc, dyT, oT, wo, gq, offs, out_0, out_1):
         gate = keep.tile([P, N], F32, name="gate", tag="z", align_bytes=64)
         nc.vector.tensor_copy(gate[:], gate_window[:].indirect(offsets[:]))
         quantize_wo(1)
+        last_window = keep.tile([P, T], F32, name="window2", tag="w", align_bytes=64)
+        nc.gpsimd.memset(last_window[:], 0.0)
+        windows.append(last_window)
 
         gate_cols = keep.tile([P, BLOCKS], F32, name="gate_cols")
 

@@ -15,6 +15,7 @@ U8 = mybir.dt.uint8
 E4M3 = mybir.dt.float8_e4m3fn_x4
 E5M2 = mybir.dt.float8_e5m2_x4
 MULT = mybir.AluOpType.mult
+ADD = mybir.AluOpType.add
 COPY = mybir.ActivationFunctionType.Copy
 
 P = 128
@@ -29,7 +30,6 @@ WO_LOADS = [(0, 128), (128, 256), (256, 512)]
 WO_TILES = [(0, 0), (1, 0), (2, 0), (2, 128)]
 WORDS_TAGS = ("z", "w", "x", "y")
 CODES_TAGS = ("x", "y", "u", "v")
-TERMS_TAGS = ("x", "y", "q2", "q3")
 
 
 def tile_attend_gdelta_kernel(tc, dyT, oT, wo, gq, offs, out_0, out_1):
@@ -56,12 +56,12 @@ def tile_attend_gdelta_kernel(tc, dyT, oT, wo, gq, offs, out_0, out_1):
         for j in range(TILES):
             nc.sync.dma_start(o_tiles[j][:], oT[j * P : (j + 1) * P, :])
 
-        windows = [keep.tile([P, T], F32, name=f"window{w}") for w in range(WINDOWS - 1)]
+        windows = [keep.tile([P, T], F32, name=f"window{w}", tag=f"window{w}", align_bytes=64) for w in range(WINDOWS - 1)]
         nc.vector.memset(windows[0][:], 0.0)
         identity = keep.tile([P, P], F32, name="identity")
         make_identity(nc, identity[:])
         nc.gpsimd.memset(windows[1][:], 0.0)
-        delta_cols = keep.tile([P, P], F32, name="delta_cols")
+        delta_cols = keep.tile([P, QUADRANT], F32, name="delta_cols", align_bytes=64)
         nc.gpsimd.memset(delta_cols[:], 0.0)
 
         dy_words = keep.tile([P, N, PACK], BF16, name="dy_words", align_bytes=64)
@@ -141,13 +141,19 @@ def tile_attend_gdelta_kernel(tc, dyT, oT, wo, gq, offs, out_0, out_1):
             nc.vector.tensor_tensor(window[:].indirect(offsets[:]), b[j][:], gate[:], MULT)
             nc.sync.dma_start(out_0[j * P : (j + 1) * P, :], window[:])
 
-        def add_to_delta(j):
-            q = keep.tile([P, N], F32, name=f"q{j}", tag=TERMS_TAGS[j], align_bytes=64)
-            nc.vector.tensor_tensor(q[:], o_tiles[j][:].indirect(offsets[:]), b[j][:], MULT)
-            for c in range(BLOCKS):
+        def add_to_delta(j, first, last, tag):
+            width = (last - first) * P
+            q = keep.tile([P, width], F32, name=f"q{j}_{first}", tag=tag, align_bytes=64)
+            nc.vector.tensor_tensor(
+                q[:],
+                o_tiles[j][:].indirect(offsets[:, first * P // 16 : last * P // 16]),
+                b[j][:, first * P : last * P],
+                MULT,
+            )
+            for c in range(first, last):
                 nc.tensor.matmul(
                     sums[c][:],
-                    q[:, c * P : (c + 1) * P],
+                    q[:, (c - first) * P : (c - first + 1) * P],
                     identity[:],
                     start=(j == 0),
                     stop=(j == TILES - 1),
@@ -159,19 +165,28 @@ def tile_attend_gdelta_kernel(tc, dyT, oT, wo, gq, offs, out_0, out_1):
         quantize_wo(2)
         quantize_wo(3)
         turn_gates()
-        add_to_delta(0)
-        add_to_delta(1)
-        for j in (2, 3):
-            product_and_scatter(j)
-            add_to_delta(j)
+        add_to_delta(0, 0, BLOCKS, "x")
+        add_to_delta(1, 0, BLOCKS, "y")
+        product_and_scatter(2)
+        add_to_delta(2, 0, BLOCKS, "q2")
+        product_and_scatter(3)
+        add_to_delta(3, 0, 2, "q3")
+        add_to_delta(3, 2, BLOCKS, "window1")
 
         gated = keep.tile([P, BLOCKS, P], F32, name="gated")
-        for c in range(BLOCKS):
+        for c in range(BLOCKS - 1):
             nc.scalar.activation(
                 gated[:, c, :], sums[c][:], COPY, scale=gate_cols[:, c : c + 1], accum_out=delta_cols[:, c : c + 1]
             )
-        delta_turned = psum_b.tile([P, P], F32, name="delta_turned", tag="ring")
-        nc.tensor.transpose(delta_turned[:], delta_cols[:], identity[:])
-        delta_rows = keep.tile([QUADRANT, P], F32, name="delta_rows")
-        nc.scalar.copy(delta_rows[:], delta_turned[0:QUADRANT, :])
-        nc.scalar.dma_start(out_1.rearrange("o (c p) -> (o c) p", p=P), delta_rows[0:BLOCKS, :])
+        c = BLOCKS - 1
+        nc.vector.tensor_scalar(
+            gated[:, c, :], sums[c][:], gate_cols[:, c : c + 1], None, MULT, ADD, accum_out=delta_cols[:, c : c + 1]
+        )
+        delta_rows = keep.tile([P, QUADRANT], F32, name="delta_rows", align_bytes=64)
+        nc.vector.transpose(delta_rows[:], delta_cols[:])
+        for c in range(BLOCKS):
+            queue = nc.scalar if c >= 2 else nc.sync
+            queue.dma_start(
+                out_1[:, c * P : (c + 1) * P].rearrange("o (q r) -> (o q) r", r=QUADRANT),
+                delta_rows[c : P : QUADRANT, :],
+            )

@@ -27,9 +27,8 @@ LINE = 4
 QUADRANT = 32
 WINDOWS = 3
 WO_LOADS = [(0, 128), (128, 256), (256, 512)]
-WO_TILES = [(0, 0), (1, 0), (2, 0), (2, 128)]
-WORDS_TAGS = ("z", "w", "x", "y")
-CODES_TAGS = ("x", "y", "u", "v")
+WORDS_TAGS = ("z", "w", "x")
+CODES_TAGS = ("x", "y", "u")
 
 
 def tile_attend_gdelta_kernel(tc, dyT, oT, wo, gq, offs, out_0, out_1):
@@ -61,8 +60,9 @@ def tile_attend_gdelta_kernel(tc, dyT, oT, wo, gq, offs, out_0, out_1):
         identity = keep.tile([P, P], F32, name="identity")
         make_identity(nc, identity[:])
         nc.gpsimd.memset(windows[1][:], 0.0)
-        delta_cols = keep.tile([P, QUADRANT], F32, name="delta_cols", align_bytes=64)
-        nc.gpsimd.memset(delta_cols[:], 0.0)
+        delta_cols = [keep.tile([P, QUADRANT], F32, name=f"delta_cols{h}", align_bytes=64) for h in range(2)]
+        for cols in delta_cols:
+            nc.gpsimd.memset(cols[:], 0.0)
 
         dy_words = keep.tile([P, N, PACK], BF16, name="dy_words", align_bytes=64)
 
@@ -80,30 +80,40 @@ def tile_attend_gdelta_kernel(tc, dyT, oT, wo, gq, offs, out_0, out_1):
                 COPY,
             )
 
-        for t in range(PACK):
+        for t in range(PACK - 1):
             nc.vector.tensor_copy(dy_words[:, :, t], dy_planes[t][:].indirect(offsets[:]))
+        halves = [slice(0, N // 2), slice(N // 2, N)]
+        for half in halves:
+            nc.vector.tensor_copy(
+                dy_words[:, half, PACK - 1],
+                dy_planes[PACK - 1][:].indirect(offsets[:, half.start // 16 : half.stop // 16]),
+            )
 
         dy_codes = keep.tile([P, N], U32, name="dy_codes", align_bytes=64)
         dy_scales = keep.tile([P, N], U8, name="dy_scales", align_bytes=64)
-        nc.vector.quantize_mx(
-            out=dy_codes[:].bitcast(E5M2), scales=dy_scales[:], in_=dy_words[:].rearrange("p n t -> p (n t)")
-        )
+        for half in halves:
+            nc.vector.quantize_mx(
+                out=dy_codes[:, half].bitcast(E5M2),
+                scales=dy_scales[:, half],
+                in_=dy_words[:, half, :].rearrange("p n t -> p (n t)"),
+            )
 
         stationary = []
 
-        def quantize_wo(j):
-            load, lo = WO_TILES[j]
-            wo_words = keep.tile([P, P, PACK], BF16, name=f"wo_words{j}", tag=WORDS_TAGS[j], align_bytes=64)
+        def quantize_wo(load):
+            lo, hi = WO_LOADS[load]
+            wo_words = keep.tile([P, hi - lo, PACK], BF16, name=f"wo_words{load}", tag=WORDS_TAGS[load], align_bytes=64)
             nc.scalar.copy(
                 wo_words[:].rearrange("p (c i) t -> p c t i", i=LINE),
-                wo_raw[load][:, :, lo : lo + P].rearrange("p t (c i) -> p c t i", i=LINE),
+                wo_raw[load][:].rearrange("p t (c i) -> p c t i", i=LINE),
             )
-            wo_codes = keep.tile([P, P], U32, name=f"wo_codes{j}", tag=CODES_TAGS[j], align_bytes=64)
-            wo_scales = keep.tile([P, P], U8, name=f"wo_scales{j}", align_bytes=64)
+            wo_codes = keep.tile([P, hi - lo], U32, name=f"wo_codes{load}", tag=CODES_TAGS[load], align_bytes=64)
+            wo_scales = keep.tile([P, hi - lo], U8, name=f"wo_scales{load}", align_bytes=64)
             nc.vector.quantize_mx(
                 out=wo_codes[:].bitcast(E4M3), scales=wo_scales[:], in_=wo_words[:].rearrange("p c t -> p (c t)")
             )
-            stationary.append((wo_codes, wo_scales))
+            for k in range(0, hi - lo, P):
+                stationary.append((wo_codes[:, k : k + P], wo_scales[:, k : k + P]))
 
         quantize_wo(0)
         gate = keep.tile([P, N], F32, name="gate", tag="z", align_bytes=64)
@@ -129,8 +139,8 @@ def tile_attend_gdelta_kernel(tc, dyT, oT, wo, gq, offs, out_0, out_1):
             bank = psum_b.tile([P, N], F32, name="bank", tag="ring")
             nc.tensor.matmul_mx(
                 out=bank[:],
-                lhsT=wo_codes[:].bitcast(E4M3),
-                lhsT_scale=wo_scales[:],
+                lhsT=wo_codes.bitcast(E4M3),
+                lhsT_scale=wo_scales,
                 rhs=dy_codes[:].bitcast(E5M2),
                 rhs_scale=dy_scales[:],
                 start=True,
@@ -141,11 +151,9 @@ def tile_attend_gdelta_kernel(tc, dyT, oT, wo, gq, offs, out_0, out_1):
             nc.vector.tensor_tensor(window[:].indirect(offsets[:]), b[j][:], gate[:], MULT)
             nc.sync.dma_start(out_0[j * P : (j + 1) * P, :], window[:])
 
-        def add_to_delta(j, first, last, tag):
-            width = (last - first) * P
-            q = keep.tile([P, width], F32, name=f"q{j}_{first}", tag=tag, align_bytes=64)
+        def add_to_delta(j, first, last, q):
             nc.vector.tensor_tensor(
-                q[:],
+                q,
                 o_tiles[j][:].indirect(offsets[:, first * P // 16 : last * P // 16]),
                 b[j][:, first * P : last * P],
                 MULT,
@@ -163,30 +171,34 @@ def tile_attend_gdelta_kernel(tc, dyT, oT, wo, gq, offs, out_0, out_1):
         product_and_scatter(0)
         product_and_scatter(1)
         quantize_wo(2)
-        quantize_wo(3)
         turn_gates()
-        add_to_delta(0, 0, BLOCKS, "x")
-        add_to_delta(1, 0, BLOCKS, "y")
+        add_to_delta(0, 0, BLOCKS, keep.tile([P, N], F32, name="q0", tag="x", align_bytes=64)[:])
+        add_to_delta(1, 0, BLOCKS, keep.tile([P, N], F32, name="q1", tag="y", align_bytes=64)[:])
         product_and_scatter(2)
-        add_to_delta(2, 0, BLOCKS, "q2")
+        add_to_delta(2, 0, BLOCKS, keep.tile([P, N], F32, name="q2")[:])
         product_and_scatter(3)
-        add_to_delta(3, 0, 2, "q3")
-        add_to_delta(3, 2, BLOCKS, "window1")
+        add_to_delta(3, 0, 2, keep.tile([P, N // 2], F32, name="q3")[:])
+        late = keep.tile([P, N // 2 + QUADRANT], F32, name="late", tag="window1", align_bytes=64)
+        add_to_delta(3, 2, BLOCKS, late[:, 0 : N // 2])
+        last_rows = keep.tile([P, QUADRANT], F32, name="last_rows", align_bytes=64)
+        rows = [late[:, N // 2 :], last_rows[:]]
 
         gated = keep.tile([P, BLOCKS, P], F32, name="gated")
-        for c in range(BLOCKS - 1):
-            nc.scalar.activation(
-                gated[:, c, :], sums[c][:], COPY, scale=gate_cols[:, c : c + 1], accum_out=delta_cols[:, c : c + 1]
-            )
-        c = BLOCKS - 1
-        nc.vector.tensor_scalar(
-            gated[:, c, :], sums[c][:], gate_cols[:, c : c + 1], None, MULT, ADD, accum_out=delta_cols[:, c : c + 1]
-        )
-        delta_rows = keep.tile([P, QUADRANT], F32, name="delta_rows", align_bytes=64)
-        nc.vector.transpose(delta_rows[:], delta_cols[:])
-        for c in range(BLOCKS):
-            queue = nc.scalar if c >= 2 else nc.sync
-            queue.dma_start(
-                out_1[:, c * P : (c + 1) * P].rearrange("o (q r) -> (o q) r", r=QUADRANT),
-                delta_rows[c : P : QUADRANT, :],
-            )
+        for h in range(2):
+            for k in range(2):
+                c = 2 * h + k
+                column = delta_cols[h][:, k : k + 1]
+                if c < BLOCKS - 1:
+                    nc.scalar.activation(gated[:, c, :], sums[c][:], COPY, scale=gate_cols[:, c : c + 1], accum_out=column)
+                else:
+                    nc.vector.tensor_scalar(
+                        gated[:, c, :], sums[c][:], gate_cols[:, c : c + 1], None, MULT, ADD, accum_out=column
+                    )
+            delta_rows = rows[h]
+            nc.vector.transpose(delta_rows, delta_cols[h][:])
+            for k, queue in enumerate((nc.scalar if h else nc.sync, nc.sync)):
+                c = 2 * h + k
+                queue.dma_start(
+                    out_1[:, c * P : (c + 1) * P].rearrange("o (q r) -> (o q) r", r=QUADRANT),
+                    delta_rows[k : P : QUADRANT, :],
+                )

@@ -27,8 +27,8 @@ LINE = 4
 QUADRANT = 32
 WINDOWS = 3
 WO_LOADS = [(0, 128), (128, 256), (256, 512)]
-WORDS_TAGS = ("z", "w", "x")
-CODES_TAGS = ("x", "y", "u")
+WORDS_TAGS = ("early", "raw0", "early")
+CODES_TAGS = ("x", "y", "x")
 
 
 def tile_attend_gdelta_kernel(tc, dyT, oT, wo, gq, offs, out_0, out_1):
@@ -41,7 +41,7 @@ def tile_attend_gdelta_kernel(tc, dyT, oT, wo, gq, offs, out_0, out_1):
         offsets = keep.tile([P, N // 16], U16, name="offsets")
         dy_planes = [keep.tile([P, T], F32, name=f"dy{t}") for t in range(PACK)]
         o_tiles = [keep.tile([P, T], F32, name=f"o{j}") for j in range(TILES)]
-        wo_raw = [keep.tile([P, PACK, hi - lo], F32, name=f"wo_raw{lo}") for lo, hi in WO_LOADS]
+        wo_raw = [keep.tile([P, PACK, hi - lo], F32, name=f"wo_raw{lo}", tag=f"raw{lo}", align_bytes=64) for lo, hi in WO_LOADS]
         dy_rows = dyT.rearrange("(p t) n -> t p n", t=PACK)
 
         gate_runs = keep.tile([P, RUN], F32, name="gate_runs")
@@ -59,14 +59,12 @@ def tile_attend_gdelta_kernel(tc, dyT, oT, wo, gq, offs, out_0, out_1):
         nc.vector.memset(windows[0][:], 0.0)
         identity = keep.tile([P, P], F32, name="identity")
         make_identity(nc, identity[:])
-        nc.gpsimd.memset(windows[1][:], 0.0)
+        nc.vector.memset(windows[1][:], 0.0)
         delta_cols = [keep.tile([P, QUADRANT], F32, name=f"delta_cols{h}", align_bytes=64) for h in range(2)]
         for cols in delta_cols:
             nc.gpsimd.memset(cols[:], 0.0)
 
-        dy_words = keep.tile([P, N, PACK], BF16, name="dy_words", align_bytes=64)
-
-        gate_window = keep.tile([P, T], F32, name="gate_window")
+        gate_window = keep.tile([P, T], F32, name="gate_window", tag="gates", align_bytes=64)
         for a in range(RUN // BLOCKS):
             spread = psum.tile([P, BLOCKS, P], F32, name=f"spread{a}", tag=f"bank{a}")
             for u in range(BLOCKS):
@@ -80,8 +78,14 @@ def tile_attend_gdelta_kernel(tc, dyT, oT, wo, gq, offs, out_0, out_1):
                 COPY,
             )
 
-        for t in range(PACK - 1):
-            nc.vector.tensor_copy(dy_words[:, :, t], dy_planes[t][:].indirect(offsets[:]))
+        gate = keep.tile([P, N], F32, name="gate")
+        nc.vector.tensor_copy(gate[:], gate_window[:].indirect(offsets[:]))
+        dy_words = keep.tile([P, N, PACK], BF16, name="dy_words", tag="gates", align_bytes=64)
+        dy_early = keep.tile([P, 2, N], BF16, name="dy_early", tag="early", align_bytes=64)
+        for t in range(2):
+            nc.vector.tensor_copy(dy_early[:, t, :], dy_planes[t][:].indirect(offsets[:]))
+        nc.scalar.copy(dy_words[:, :, 0:2], dy_early[:].rearrange("p t n -> p n t"))
+        nc.vector.tensor_copy(dy_words[:, :, 2], dy_planes[2][:].indirect(offsets[:]))
         halves = [slice(0, N // 2), slice(N // 2, N)]
         for half in halves:
             nc.vector.tensor_copy(
@@ -100,13 +104,18 @@ def tile_attend_gdelta_kernel(tc, dyT, oT, wo, gq, offs, out_0, out_1):
 
         stationary = []
 
-        def quantize_wo(load):
+        def lay_out_wo(load):
             lo, hi = WO_LOADS[load]
             wo_words = keep.tile([P, hi - lo, PACK], BF16, name=f"wo_words{load}", tag=WORDS_TAGS[load], align_bytes=64)
-            nc.scalar.copy(
-                wo_words[:].rearrange("p (c i) t -> p c t i", i=LINE),
-                wo_raw[load][:].rearrange("p t (c i) -> p c t i", i=LINE),
-            )
+            for k in range(0, hi - lo, P):
+                (nc.vector.tensor_copy if k else nc.scalar.copy)(
+                    wo_words[:, k : k + P, :].rearrange("p (c i) t -> p c t i", i=LINE),
+                    wo_raw[load][:, :, k : k + P].rearrange("p t (c i) -> p c t i", i=LINE),
+                )
+            return wo_words
+
+        def quantize_wo(load, wo_words):
+            lo, hi = WO_LOADS[load]
             wo_codes = keep.tile([P, hi - lo], U32, name=f"wo_codes{load}", tag=CODES_TAGS[load], align_bytes=64)
             wo_scales = keep.tile([P, hi - lo], U8, name=f"wo_scales{load}", align_bytes=64)
             nc.vector.quantize_mx(
@@ -115,13 +124,9 @@ def tile_attend_gdelta_kernel(tc, dyT, oT, wo, gq, offs, out_0, out_1):
             for k in range(0, hi - lo, P):
                 stationary.append((wo_codes[:, k : k + P], wo_scales[:, k : k + P]))
 
-        quantize_wo(0)
-        gate = keep.tile([P, N], F32, name="gate", tag="z", align_bytes=64)
-        nc.vector.tensor_copy(gate[:], gate_window[:].indirect(offsets[:]))
-        quantize_wo(1)
-        last_window = keep.tile([P, T], F32, name="window2", tag="w", align_bytes=64)
-        nc.gpsimd.memset(last_window[:], 0.0)
-        windows.append(last_window)
+        quantize_wo(0, lay_out_wo(0))
+        quantize_wo(1, lay_out_wo(1))
+        rest_words = lay_out_wo(2)
 
         gate_cols = keep.tile([P, BLOCKS], F32, name="gate_cols")
 
@@ -146,9 +151,16 @@ def tile_attend_gdelta_kernel(tc, dyT, oT, wo, gq, offs, out_0, out_1):
                 start=True,
                 stop=True,
             )
-            nc.scalar.copy(b[j][:], bank[:])
             window = windows[j % WINDOWS]
-            nc.vector.tensor_tensor(window[:].indirect(offsets[:]), b[j][:], gate[:], MULT)
+            if j == 0:
+                gated_b = keep.tile([P, N], F32, name="gated_b")
+                nc.vector.tensor_tensor(gated_b[:], bank[:], gate[:], MULT)
+                quantize_wo(2, rest_words)
+                nc.vector.tensor_copy(window[:].indirect(offsets[:]), gated_b[:])
+                nc.scalar.copy(b[j][:], bank[:])
+            else:
+                nc.scalar.copy(b[j][:], bank[:])
+                nc.vector.tensor_tensor(window[:].indirect(offsets[:]), b[j][:], gate[:], MULT)
             nc.sync.dma_start(out_0[j * P : (j + 1) * P, :], window[:])
 
         def add_to_delta(j, first, last, q):
@@ -169,8 +181,10 @@ def tile_attend_gdelta_kernel(tc, dyT, oT, wo, gq, offs, out_0, out_1):
                 )
 
         product_and_scatter(0)
+        last_window = keep.tile([P, T], F32, name="window2", tag="early", align_bytes=64)
+        nc.gpsimd.memset(last_window[:], 0.0)
+        windows.append(last_window)
         product_and_scatter(1)
-        quantize_wo(2)
         turn_gates()
         add_to_delta(0, 0, BLOCKS, keep.tile([P, N], F32, name="q0", tag="x", align_bytes=64)[:])
         add_to_delta(1, 0, BLOCKS, keep.tile([P, N], F32, name="q1", tag="y", align_bytes=64)[:])

@@ -27,8 +27,10 @@ LINE = 4
 QUADRANT = 32
 WINDOWS = 3
 WO_LOADS = [(0, 128), (128, 256), (256, 512)]
-WORDS_TAGS = ("early", "raw0", "early")
-CODES_TAGS = ("x", "y", "x")
+WORDS_TAGS = ("early", "early", "codes1")
+WINDOW_OF = (0, 1, 2, 1)
+B_TAGS = ("raw256", "b1", "b2", "b3")
+HALF = N // 2
 
 
 def tile_attend_gdelta_kernel(tc, dyT, oT, wo, gq, offs, out_0, out_1):
@@ -36,7 +38,7 @@ def tile_attend_gdelta_kernel(tc, dyT, oT, wo, gq, offs, out_0, out_1):
     with ExitStack() as ctx:
         keep = ctx.enter_context(tc.tile_pool(name="keep", bufs=1))
         psum = ctx.enter_context(tc.psum_pool(name="psum", bufs=1))
-        psum_b = ctx.enter_context(tc.psum_pool(name="psum_b", bufs=2))
+        psum_b = ctx.enter_context(tc.psum_pool(name="psum_b", bufs=3))
 
         offsets = keep.tile([P, N // 16], U16, name="offsets")
         dy_planes = [keep.tile([P, T], F32, name=f"dy{t}") for t in range(PACK)]
@@ -45,7 +47,7 @@ def tile_attend_gdelta_kernel(tc, dyT, oT, wo, gq, offs, out_0, out_1):
         dy_rows = dyT.rearrange("(p t) n -> t p n", t=PACK)
 
         gate_runs = keep.tile([P, RUN], F32, name="gate_runs")
-        nc.scalar.dma_start(gate_runs[:], gq[0:1, :].rearrange("o (p u) -> (o p) u", u=RUN))
+        nc.sync.dma_start(gate_runs[:], gq[0:1, :].rearrange("o (p u) -> (o p) u", u=RUN))
         nc.sync.dma_start(dy_planes[0][:], dy_rows[0])
         nc.sync.dma_start(offsets[:], offs)
         for t in range(1, PACK):
@@ -55,7 +57,7 @@ def tile_attend_gdelta_kernel(tc, dyT, oT, wo, gq, offs, out_0, out_1):
         for j in range(TILES):
             nc.sync.dma_start(o_tiles[j][:], oT[j * P : (j + 1) * P, :])
 
-        windows = [keep.tile([P, T], F32, name=f"window{w}", tag=f"window{w}", align_bytes=64) for w in range(WINDOWS - 1)]
+        windows = [keep.tile([P, T], F32, name=f"window{w}", tag=f"window{w}", align_bytes=64) for w in range(WINDOWS)]
         nc.vector.memset(windows[0][:], 0.0)
         identity = keep.tile([P, P], F32, name="identity")
         make_identity(nc, identity[:])
@@ -63,6 +65,11 @@ def tile_attend_gdelta_kernel(tc, dyT, oT, wo, gq, offs, out_0, out_1):
         delta_cols = [keep.tile([P, QUADRANT], F32, name=f"delta_cols{h}", align_bytes=64) for h in range(2)]
         for cols in delta_cols:
             nc.gpsimd.memset(cols[:], 0.0)
+        dy_codes = keep.tile([P, HALF + N], U32, name="dy_codes", align_bytes=64)
+        dy_scales = keep.tile([P, HALF + N], U8, name="dy_scales", align_bytes=64)
+        nc.gpsimd.memset(dy_codes[:, 0:HALF], 0)
+        nc.gpsimd.memset(dy_scales[:, 0:HALF], 0)
+        nc.gpsimd.memset(windows[2][:], 0.0)
 
         gate_window = keep.tile([P, T], F32, name="gate_window", tag="gates", align_bytes=64)
         for a in range(RUN // BLOCKS):
@@ -80,43 +87,42 @@ def tile_attend_gdelta_kernel(tc, dyT, oT, wo, gq, offs, out_0, out_1):
 
         gate = keep.tile([P, N], F32, name="gate")
         nc.vector.tensor_copy(gate[:], gate_window[:].indirect(offsets[:]))
-        dy_words = keep.tile([P, N, PACK], BF16, name="dy_words", tag="gates", align_bytes=64)
-        dy_early = keep.tile([P, 2, N], BF16, name="dy_early", tag="early", align_bytes=64)
-        for t in range(2):
-            nc.vector.tensor_copy(dy_early[:, t, :], dy_planes[t][:].indirect(offsets[:]))
-        nc.scalar.copy(dy_words[:, :, 0:2], dy_early[:].rearrange("p t n -> p n t"))
-        nc.vector.tensor_copy(dy_words[:, :, 2], dy_planes[2][:].indirect(offsets[:]))
-        halves = [slice(0, N // 2), slice(N // 2, N)]
-        for half in halves:
-            nc.vector.tensor_copy(
-                dy_words[:, half, PACK - 1],
-                dy_planes[PACK - 1][:].indirect(offsets[:, half.start // 16 : half.stop // 16]),
+        lists = [offsets[:, 0 : HALF // 16], offsets[:, HALF // 16 : N // 16]]
+        staged = keep.tile([P, 2 * HALF * PACK], BF16, name="staged", tag="gates", align_bytes=64)
+        words_a = staged[:, 0 : HALF * PACK].rearrange("p (n t) -> p n t", t=PACK)
+        rows_a = keep.tile([P, 2, HALF], BF16, name="rows_a", tag="early", align_bytes=64)
+        rows_b = staged[:, HALF * PACK :].rearrange("p (t n) -> p t n", t=PACK)
+        for t in range(PACK):
+            first_out = rows_a[:, t, :] if t < 2 else words_a[:, :, t]
+            nc.vector.tensor_copy(first_out, dy_planes[t][:].indirect(lists[0]))
+            if t == 1:
+                nc.scalar.copy(words_a[:, :, 0:2], rows_a[:].rearrange("p t n -> p n t"))
+            nc.vector.tensor_copy(rows_b[:, t, :], dy_planes[t][:].indirect(lists[1]))
+
+        def weave(copy, words, rows):
+            copy(
+                words.rearrange("p (c i) t -> p c t i", i=LINE),
+                rows.rearrange("p t (c i) -> p c t i", i=LINE),
             )
 
-        dy_codes = keep.tile([P, N], U32, name="dy_codes", align_bytes=64)
-        dy_scales = keep.tile([P, N], U8, name="dy_scales", align_bytes=64)
-        for half in halves:
+        def quantize_dy(lo, words):
             nc.vector.quantize_mx(
-                out=dy_codes[:, half].bitcast(E5M2),
-                scales=dy_scales[:, half],
-                in_=dy_words[:, half, :].rearrange("p n t -> p (n t)"),
+                out=dy_codes[:, lo : lo + HALF].bitcast(E5M2),
+                scales=dy_scales[:, lo : lo + HALF],
+                in_=words.rearrange("p n t -> p (n t)"),
             )
 
         stationary = []
 
-        def lay_out_wo(load):
+        def lay_out_wo(load, copy):
             lo, hi = WO_LOADS[load]
             wo_words = keep.tile([P, hi - lo, PACK], BF16, name=f"wo_words{load}", tag=WORDS_TAGS[load], align_bytes=64)
-            for k in range(0, hi - lo, P):
-                (nc.vector.tensor_copy if k else nc.scalar.copy)(
-                    wo_words[:, k : k + P, :].rearrange("p (c i) t -> p c t i", i=LINE),
-                    wo_raw[load][:, :, k : k + P].rearrange("p t (c i) -> p c t i", i=LINE),
-                )
+            weave(copy, wo_words[:], wo_raw[load][:])
             return wo_words
 
         def quantize_wo(load, wo_words):
             lo, hi = WO_LOADS[load]
-            wo_codes = keep.tile([P, hi - lo], U32, name=f"wo_codes{load}", tag=CODES_TAGS[load], align_bytes=64)
+            wo_codes = keep.tile([P, hi - lo], U32, name=f"wo_codes{load}", tag=f"codes{load}", align_bytes=64)
             wo_scales = keep.tile([P, hi - lo], U8, name=f"wo_scales{load}", align_bytes=64)
             nc.vector.quantize_mx(
                 out=wo_codes[:].bitcast(E4M3), scales=wo_scales[:], in_=wo_words[:].rearrange("p c t -> p (c t)")
@@ -124,9 +130,30 @@ def tile_attend_gdelta_kernel(tc, dyT, oT, wo, gq, offs, out_0, out_1):
             for k in range(0, hi - lo, P):
                 stationary.append((wo_codes[:, k : k + P], wo_scales[:, k : k + P]))
 
-        quantize_wo(0, lay_out_wo(0))
-        quantize_wo(1, lay_out_wo(1))
-        rest_words = lay_out_wo(2)
+        def product(j, lo):
+            wo_codes, wo_scales = stationary[j]
+            bank = psum_b.tile([P, N], F32, name="bank", tag="ring")
+            nc.tensor.matmul_mx(
+                out=bank[:],
+                lhsT=wo_codes.bitcast(E4M3),
+                lhsT_scale=wo_scales,
+                rhs=dy_codes[:, lo : lo + N].bitcast(E5M2),
+                rhs_scale=dy_scales[:, lo : lo + N],
+                start=True,
+                stop=True,
+            )
+            return bank
+
+        quantize_dy(HALF, words_a)
+        quantize_wo(0, lay_out_wo(0, nc.scalar.copy))
+        early_bank = product(0, 0)
+        words_b = keep.tile([P, HALF, PACK], BF16, name="words_b", tag="raw0", align_bytes=64)
+        weave(nc.vector.tensor_copy, words_b[:], rows_b)
+        quantize_wo(1, lay_out_wo(1, nc.scalar.copy))
+        quantize_dy(N, words_b[:])
+        early_b = keep.tile([P, HALF], F32, name="early_b")
+        nc.scalar.copy(early_b[:], early_bank[:, HALF:N])
+        nc.vector.tensor_tensor(windows[0][:].indirect(lists[0]), early_b[:], gate[:, 0:HALF], MULT)
 
         gate_cols = keep.tile([P, BLOCKS], F32, name="gate_cols")
 
@@ -137,30 +164,14 @@ def tile_attend_gdelta_kernel(tc, dyT, oT, wo, gq, offs, out_0, out_1):
             nc.scalar.copy(gate_cols[:], turned[:, :, 0])
 
         sums = [psum.tile([P, P], F32, name=f"sums{c}", tag=f"bank{c}") for c in range(BLOCKS)]
-        b = [keep.tile([P, N], F32, name=f"b{j}") for j in range(TILES)]
+        b = [keep.tile([P, N], F32, name=f"b{j}", tag=B_TAGS[j], align_bytes=64) for j in range(TILES)]
 
         def product_and_scatter(j):
-            wo_codes, wo_scales = stationary[j]
-            bank = psum_b.tile([P, N], F32, name="bank", tag="ring")
-            nc.tensor.matmul_mx(
-                out=bank[:],
-                lhsT=wo_codes.bitcast(E4M3),
-                lhsT_scale=wo_scales,
-                rhs=dy_codes[:].bitcast(E5M2),
-                rhs_scale=dy_scales[:],
-                start=True,
-                stop=True,
-            )
-            window = windows[j % WINDOWS]
-            if j == 0:
-                gated_b = keep.tile([P, N], F32, name="gated_b")
-                nc.vector.tensor_tensor(gated_b[:], bank[:], gate[:], MULT)
-                quantize_wo(2, rest_words)
-                nc.vector.tensor_copy(window[:].indirect(offsets[:]), gated_b[:])
-                nc.scalar.copy(b[j][:], bank[:])
-            else:
-                nc.scalar.copy(b[j][:], bank[:])
-                nc.vector.tensor_tensor(window[:].indirect(offsets[:]), b[j][:], gate[:], MULT)
+            bank = product(j, HALF)
+            window = windows[WINDOW_OF[j]]
+            nc.scalar.copy(b[j][:], bank[:])
+            lo = HALF if j == 0 else 0
+            nc.vector.tensor_tensor(window[:].indirect(offsets[:, lo // 16 :]), b[j][:, lo:], gate[:, lo:], MULT)
             nc.sync.dma_start(out_0[j * P : (j + 1) * P, :], window[:])
 
         def add_to_delta(j, first, last, q):
@@ -180,19 +191,17 @@ def tile_attend_gdelta_kernel(tc, dyT, oT, wo, gq, offs, out_0, out_1):
                     is_transpose=True,
                 )
 
-        product_and_scatter(0)
-        last_window = keep.tile([P, T], F32, name="window2", tag="early", align_bytes=64)
-        nc.gpsimd.memset(last_window[:], 0.0)
-        windows.append(last_window)
         product_and_scatter(1)
+        quantize_wo(2, lay_out_wo(2, nc.scalar.copy))
+        product_and_scatter(0)
         turn_gates()
-        add_to_delta(0, 0, BLOCKS, keep.tile([P, N], F32, name="q0", tag="x", align_bytes=64)[:])
-        add_to_delta(1, 0, BLOCKS, keep.tile([P, N], F32, name="q1", tag="y", align_bytes=64)[:])
+        add_to_delta(0, 0, BLOCKS, keep.tile([P, N], F32, name="q0")[:])
+        add_to_delta(1, 0, BLOCKS, keep.tile([P, N], F32, name="q1")[:])
         product_and_scatter(2)
         add_to_delta(2, 0, BLOCKS, keep.tile([P, N], F32, name="q2")[:])
         product_and_scatter(3)
         add_to_delta(3, 0, 2, keep.tile([P, N // 2], F32, name="q3")[:])
-        late = keep.tile([P, N // 2 + QUADRANT], F32, name="late", tag="window1", align_bytes=64)
+        late = keep.tile([P, N // 2 + QUADRANT], F32, name="late", tag="window0", align_bytes=64)
         add_to_delta(3, 2, BLOCKS, late[:, 0 : N // 2])
         last_rows = keep.tile([P, QUADRANT], F32, name="last_rows", align_bytes=64)
         rows = [late[:, N // 2 :], last_rows[:]]

@@ -27,9 +27,9 @@ LINE = 4
 QUADRANT = 32
 WINDOWS = 3
 WO_LOADS = [(0, 128), (128, 256), (256, 512)]
-WORDS_TAGS = ("early", "early", "codes1")
-WINDOW_OF = (0, 1, 2, 1)
-B_TAGS = ("raw256", "b1", "b2", "b3")
+WORDS_TAGS = ("early", "gates", "codes0")
+WINDOW_OF = (0, 1, 2, 0)
+BANK_OF = ("ring1", "ring0", "ring1", "ring0")
 HALF = N // 2
 
 
@@ -38,7 +38,7 @@ def tile_attend_gdelta_kernel(tc, dyT, oT, wo, gq, offs, out_0, out_1):
     with ExitStack() as ctx:
         keep = ctx.enter_context(tc.tile_pool(name="keep", bufs=1))
         psum = ctx.enter_context(tc.psum_pool(name="psum", bufs=1))
-        psum_b = ctx.enter_context(tc.psum_pool(name="psum_b", bufs=3))
+        psum_b = ctx.enter_context(tc.psum_pool(name="psum_b", bufs=1))
 
         offsets = keep.tile([P, N // 16], U16, name="offsets")
         dy_planes = [keep.tile([P, T], F32, name=f"dy{t}") for t in range(PACK)]
@@ -47,7 +47,7 @@ def tile_attend_gdelta_kernel(tc, dyT, oT, wo, gq, offs, out_0, out_1):
         dy_rows = dyT.rearrange("(p t) n -> t p n", t=PACK)
 
         gate_runs = keep.tile([P, RUN], F32, name="gate_runs")
-        nc.sync.dma_start(gate_runs[:], gq[0:1, :].rearrange("o (p u) -> (o p) u", u=RUN))
+        nc.scalar.dma_start(gate_runs[:], gq[0:1, :].rearrange("o (p u) -> (o p) u", u=RUN))
         nc.sync.dma_start(dy_planes[0][:], dy_rows[0])
         nc.sync.dma_start(offsets[:], offs)
         for t in range(1, PACK):
@@ -88,16 +88,13 @@ def tile_attend_gdelta_kernel(tc, dyT, oT, wo, gq, offs, out_0, out_1):
         gate = keep.tile([P, N], F32, name="gate")
         nc.vector.tensor_copy(gate[:], gate_window[:].indirect(offsets[:]))
         lists = [offsets[:, 0 : HALF // 16], offsets[:, HALF // 16 : N // 16]]
-        staged = keep.tile([P, 2 * HALF * PACK], BF16, name="staged", tag="gates", align_bytes=64)
-        words_a = staged[:, 0 : HALF * PACK].rearrange("p (n t) -> p n t", t=PACK)
-        rows_a = keep.tile([P, 2, HALF], BF16, name="rows_a", tag="early", align_bytes=64)
-        rows_b = staged[:, HALF * PACK :].rearrange("p (t n) -> p t n", t=PACK)
-        for t in range(PACK):
-            first_out = rows_a[:, t, :] if t < 2 else words_a[:, :, t]
-            nc.vector.tensor_copy(first_out, dy_planes[t][:].indirect(lists[0]))
-            if t == 1:
-                nc.scalar.copy(words_a[:, :, 0:2], rows_a[:].rearrange("p t n -> p n t"))
-            nc.vector.tensor_copy(rows_b[:, t, :], dy_planes[t][:].indirect(lists[1]))
+        dy_words = keep.tile([P, N, PACK], BF16, name="dy_words", tag="gates", align_bytes=64)
+        dy_early = keep.tile([P, 2, N], BF16, name="dy_early", tag="early", align_bytes=64)
+        for t in range(2):
+            nc.vector.tensor_copy(dy_early[:, t, :], dy_planes[t][:].indirect(offsets[:]))
+        nc.scalar.copy(dy_words[:, :, 0:2], dy_early[:].rearrange("p t n -> p n t"))
+        nc.vector.tensor_copy(dy_words[:, :, 2], dy_planes[2][:].indirect(offsets[:]))
+        nc.vector.tensor_copy(dy_words[:, 0:HALF, 3], dy_planes[3][:].indirect(lists[0]))
 
         def weave(copy, words, rows):
             copy(
@@ -105,11 +102,11 @@ def tile_attend_gdelta_kernel(tc, dyT, oT, wo, gq, offs, out_0, out_1):
                 rows.rearrange("p t (c i) -> p c t i", i=LINE),
             )
 
-        def quantize_dy(lo, words):
+        def quantize_dy(lo, count):
             nc.vector.quantize_mx(
-                out=dy_codes[:, lo : lo + HALF].bitcast(E5M2),
-                scales=dy_scales[:, lo : lo + HALF],
-                in_=words.rearrange("p n t -> p (n t)"),
+                out=dy_codes[:, HALF + lo : HALF + lo + count].bitcast(E5M2),
+                scales=dy_scales[:, HALF + lo : HALF + lo + count],
+                in_=dy_words[:, lo : lo + count, :].rearrange("p n t -> p (n t)"),
             )
 
         stationary = []
@@ -130,9 +127,9 @@ def tile_attend_gdelta_kernel(tc, dyT, oT, wo, gq, offs, out_0, out_1):
             for k in range(0, hi - lo, P):
                 stationary.append((wo_codes[:, k : k + P], wo_scales[:, k : k + P]))
 
-        def product(j, lo):
+        def product(j, lo, tag):
             wo_codes, wo_scales = stationary[j]
-            bank = psum_b.tile([P, N], F32, name="bank", tag="ring")
+            bank = psum_b.tile([P, N], F32, name="bank", tag=tag)
             nc.tensor.matmul_mx(
                 out=bank[:],
                 lhsT=wo_codes.bitcast(E4M3),
@@ -144,33 +141,39 @@ def tile_attend_gdelta_kernel(tc, dyT, oT, wo, gq, offs, out_0, out_1):
             )
             return bank
 
-        quantize_dy(HALF, words_a)
-        quantize_wo(0, lay_out_wo(0, nc.scalar.copy))
-        early_bank = product(0, 0)
-        words_b = keep.tile([P, HALF, PACK], BF16, name="words_b", tag="raw0", align_bytes=64)
-        weave(nc.vector.tensor_copy, words_b[:], rows_b)
+        first_words = lay_out_wo(0, nc.vector.tensor_copy)
+        quantize_dy(0, HALF)
+        quantize_wo(0, first_words)
+        early_bank = product(0, 0, "ring0")
+        last_row = keep.tile([P, HALF], BF16, name="last_row", tag="raw0", align_bytes=64)
+        for lo in (0, P):
+            nc.vector.tensor_copy(
+                last_row[:, lo : lo + P], dy_planes[3][:].indirect(offsets[:, (HALF + lo) // 16 : (HALF + lo + P) // 16])
+            )
+        for lo in (0, P):
+            nc.vector.tensor_copy(dy_words[:, HALF + lo : HALF + lo + P, 3], last_row[:, lo : lo + P])
+        for lo in (HALF, HALF + P):
+            quantize_dy(lo, P)
+        b = [keep.tile([P, N], F32, name=f"b{j}") for j in range(TILES)]
+        nc.scalar.copy(b[0][:, 0:HALF], early_bank[:, HALF:N])
+        nc.vector.tensor_tensor(windows[0][:].indirect(lists[0]), b[0][:, 0:HALF], gate[:, 0:HALF], MULT)
         quantize_wo(1, lay_out_wo(1, nc.scalar.copy))
-        quantize_dy(N, words_b[:])
-        early_b = keep.tile([P, HALF], F32, name="early_b")
-        nc.scalar.copy(early_b[:], early_bank[:, HALF:N])
-        nc.vector.tensor_tensor(windows[0][:].indirect(lists[0]), early_b[:], gate[:, 0:HALF], MULT)
 
         gate_cols = keep.tile([P, BLOCKS], F32, name="gate_cols")
 
         def turn_gates():
-            turned = psum_b.tile([P, BLOCKS, P], F32, name="turned", tag="ring")
+            turned = psum_b.tile([P, BLOCKS, P], F32, name="turned", tag="ring0")
             for c in range(BLOCKS):
                 nc.tensor.transpose(turned[:, c, :], gate[:, c * P : (c + 1) * P], identity[:])
             nc.scalar.copy(gate_cols[:], turned[:, :, 0])
 
         sums = [psum.tile([P, P], F32, name=f"sums{c}", tag=f"bank{c}") for c in range(BLOCKS)]
-        b = [keep.tile([P, N], F32, name=f"b{j}", tag=B_TAGS[j], align_bytes=64) for j in range(TILES)]
 
         def product_and_scatter(j):
-            bank = product(j, HALF)
+            bank = product(j, HALF, BANK_OF[j])
             window = windows[WINDOW_OF[j]]
-            nc.scalar.copy(b[j][:], bank[:])
             lo = HALF if j == 0 else 0
+            nc.scalar.copy(b[j][:, lo:], bank[:, lo:])
             nc.vector.tensor_tensor(window[:].indirect(offsets[:, lo // 16 :]), b[j][:, lo:], gate[:, lo:], MULT)
             nc.sync.dma_start(out_0[j * P : (j + 1) * P, :], window[:])
 
@@ -191,9 +194,9 @@ def tile_attend_gdelta_kernel(tc, dyT, oT, wo, gq, offs, out_0, out_1):
                     is_transpose=True,
                 )
 
-        product_and_scatter(1)
-        quantize_wo(2, lay_out_wo(2, nc.scalar.copy))
         product_and_scatter(0)
+        quantize_wo(2, lay_out_wo(2, nc.scalar.copy))
+        product_and_scatter(1)
         turn_gates()
         add_to_delta(0, 0, BLOCKS, keep.tile([P, N], F32, name="q0")[:])
         add_to_delta(1, 0, BLOCKS, keep.tile([P, N], F32, name="q1")[:])
@@ -201,7 +204,7 @@ def tile_attend_gdelta_kernel(tc, dyT, oT, wo, gq, offs, out_0, out_1):
         add_to_delta(2, 0, BLOCKS, keep.tile([P, N], F32, name="q2")[:])
         product_and_scatter(3)
         add_to_delta(3, 0, 2, keep.tile([P, N // 2], F32, name="q3")[:])
-        late = keep.tile([P, N // 2 + QUADRANT], F32, name="late", tag="window0", align_bytes=64)
+        late = keep.tile([P, N // 2 + QUADRANT], F32, name="late", tag="window1", align_bytes=64)
         add_to_delta(3, 2, BLOCKS, late[:, 0 : N // 2])
         last_rows = keep.tile([P, QUADRANT], F32, name="last_rows", align_bytes=64)
         rows = [late[:, N // 2 :], last_rows[:]]

@@ -27,7 +27,8 @@ LINE = 4
 QUADRANT = 32
 WINDOWS = 3
 WO_LOADS = [(0, 128), (128, 256), (256, 512)]
-WORDS_TAGS = ("early", "gates", "codes0")
+WORDS_TAGS = ("early", "raw0", "gates")
+PLACES = (2, 3, 0, 1)
 WINDOW_OF = (0, 1, 2, 0)
 BANK_OF = ("ring1", "ring0", "ring1", "ring0")
 HALF = N // 2
@@ -48,10 +49,10 @@ def tile_attend_gdelta_kernel(tc, dyT, oT, wo, gq, offs, out_0, out_1):
 
         gate_runs = keep.tile([P, RUN], F32, name="gate_runs")
         nc.scalar.dma_start(gate_runs[:], gq[0:1, :].rearrange("o (p u) -> (o p) u", u=RUN))
-        nc.sync.dma_start(dy_planes[0][:], dy_rows[0])
+        nc.sync.dma_start(dy_planes[0][:], dy_rows[PLACES[0]])
         nc.sync.dma_start(offsets[:], offs)
         for t in range(1, PACK):
-            nc.sync.dma_start(dy_planes[t][:], dy_rows[t])
+            nc.sync.dma_start(dy_planes[t][:], dy_rows[PLACES[t]])
         for raw, (lo, hi) in zip(wo_raw, WO_LOADS):
             nc.sync.dma_start(raw[:], wo[:, lo:hi].rearrange("(p t) c -> p t c", t=PACK))
         for j in range(TILES):
@@ -88,13 +89,17 @@ def tile_attend_gdelta_kernel(tc, dyT, oT, wo, gq, offs, out_0, out_1):
         gate = keep.tile([P, N], F32, name="gate")
         nc.vector.tensor_copy(gate[:], gate_window[:].indirect(offsets[:]))
         lists = [offsets[:, 0 : HALF // 16], offsets[:, HALF // 16 : N // 16]]
-        dy_words = keep.tile([P, N, PACK], BF16, name="dy_words", tag="gates", align_bytes=64)
+        staged = keep.tile([P, N * PACK + HALF], BF16, name="staged", tag="gates", align_bytes=64)
+        dy_words = staged[:, 0 : N * PACK].rearrange("p (n t) -> p n t", t=PACK)
+        third_row = staged[:, N * PACK :]
         dy_early = keep.tile([P, 2, N], BF16, name="dy_early", tag="early", align_bytes=64)
         for t in range(2):
             nc.vector.tensor_copy(dy_early[:, t, :], dy_planes[t][:].indirect(offsets[:]))
-        nc.scalar.copy(dy_words[:, :, 0:2], dy_early[:].rearrange("p t n -> p n t"))
-        nc.vector.tensor_copy(dy_words[:, :, 2], dy_planes[2][:].indirect(offsets[:]))
-        nc.vector.tensor_copy(dy_words[:, 0:HALF, 3], dy_planes[3][:].indirect(lists[0]))
+        nc.scalar.copy(dy_words[:, :, 2:4], dy_early[:].rearrange("p t n -> p n t"))
+        nc.vector.tensor_copy(third_row, dy_planes[2][:].indirect(lists[1]))
+        nc.scalar.copy(dy_words[:, HALF:N, 0:2], third_row.unsqueeze(2).to_broadcast([P, HALF, 2]))
+        nc.vector.tensor_copy(dy_words[:, 0:HALF, 0], dy_planes[2][:].indirect(lists[0]))
+        nc.vector.tensor_copy(dy_words[:, 0:HALF, 1], dy_planes[3][:].indirect(lists[0]))
 
         def weave(copy, words, rows):
             copy(
@@ -145,19 +150,13 @@ def tile_attend_gdelta_kernel(tc, dyT, oT, wo, gq, offs, out_0, out_1):
         quantize_dy(0, HALF)
         quantize_wo(0, first_words)
         early_bank = product(0, 0, "ring0")
-        last_row = keep.tile([P, HALF], BF16, name="last_row", tag="raw0", align_bytes=64)
-        for lo in (0, P):
-            nc.vector.tensor_copy(
-                last_row[:, lo : lo + P], dy_planes[3][:].indirect(offsets[:, (HALF + lo) // 16 : (HALF + lo + P) // 16])
-            )
-        for lo in (0, P):
-            nc.vector.tensor_copy(dy_words[:, HALF + lo : HALF + lo + P, 3], last_row[:, lo : lo + P])
-        for lo in (HALF, HALF + P):
-            quantize_dy(lo, P)
+        nc.vector.tensor_copy(dy_words[:, HALF:N, 1], dy_planes[3][:].indirect(lists[1]))
+        quantize_wo(1, lay_out_wo(1, nc.scalar.copy))
+        quantize_dy(HALF, HALF)
         b = [keep.tile([P, N], F32, name=f"b{j}") for j in range(TILES)]
         nc.scalar.copy(b[0][:, 0:HALF], early_bank[:, HALF:N])
         nc.vector.tensor_tensor(windows[0][:].indirect(lists[0]), b[0][:, 0:HALF], gate[:, 0:HALF], MULT)
-        quantize_wo(1, lay_out_wo(1, nc.scalar.copy))
+        quantize_wo(2, lay_out_wo(2, nc.scalar.copy))
 
         gate_cols = keep.tile([P, BLOCKS], F32, name="gate_cols")
 
@@ -195,7 +194,6 @@ def tile_attend_gdelta_kernel(tc, dyT, oT, wo, gq, offs, out_0, out_1):
                 )
 
         product_and_scatter(0)
-        quantize_wo(2, lay_out_wo(2, nc.scalar.copy))
         product_and_scatter(1)
         turn_gates()
         add_to_delta(0, 0, BLOCKS, keep.tile([P, N], F32, name="q0")[:])

@@ -89,16 +89,16 @@ def tile_attend_gdelta_kernel(tc, dyT, oT, wo, gq, offs, out_0, out_1):
         gate = keep.tile([P, N], F32, name="gate")
         nc.vector.tensor_copy(gate[:], gate_window[:].indirect(offsets[:]))
         lists = [offsets[:, 0 : HALF // 16], offsets[:, HALF // 16 : N // 16]]
-        staged = keep.tile([P, N * PACK + HALF], BF16, name="staged", tag="gates", align_bytes=64)
+        staged = keep.tile([P, N * PACK + P], BF16, name="staged", tag="gates", align_bytes=64)
         dy_words = staged[:, 0 : N * PACK].rearrange("p (n t) -> p n t", t=PACK)
         third_row = staged[:, N * PACK :]
         dy_early = keep.tile([P, 2, N], BF16, name="dy_early", tag="early", align_bytes=64)
         for t in range(2):
             nc.vector.tensor_copy(dy_early[:, t, :], dy_planes[t][:].indirect(offsets[:]))
         nc.scalar.copy(dy_words[:, :, 2:4], dy_early[:].rearrange("p t n -> p n t"))
-        nc.vector.tensor_copy(third_row, dy_planes[2][:].indirect(lists[1]))
-        nc.scalar.copy(dy_words[:, HALF:N, 0:2], third_row.unsqueeze(2).to_broadcast([P, HALF, 2]))
-        nc.vector.tensor_copy(dy_words[:, 0:HALF, 0], dy_planes[2][:].indirect(lists[0]))
+        nc.vector.tensor_copy(third_row, dy_planes[2][:].indirect(offsets[:, 3 * P // 16 :]))
+        nc.scalar.copy(dy_words[:, 3 * P :, 0], third_row)
+        nc.vector.tensor_copy(dy_words[:, 0 : 3 * P, 0], dy_planes[2][:].indirect(offsets[:, 0 : 3 * P // 16]))
         nc.vector.tensor_copy(dy_words[:, 0:HALF, 1], dy_planes[3][:].indirect(lists[0]))
 
         def weave(copy, words, rows):
@@ -120,14 +120,14 @@ def tile_attend_gdelta_kernel(tc, dyT, oT, wo, gq, offs, out_0, out_1):
             lo, hi = WO_LOADS[load]
             wo_words = keep.tile([P, hi - lo, PACK], BF16, name=f"wo_words{load}", tag=WORDS_TAGS[load], align_bytes=64)
             weave(copy, wo_words[:], wo_raw[load][:])
-            return wo_words
+            return wo_words[:]
 
         def quantize_wo(load, wo_words):
             lo, hi = WO_LOADS[load]
             wo_codes = keep.tile([P, hi - lo], U32, name=f"wo_codes{load}", tag=f"codes{load}", align_bytes=64)
             wo_scales = keep.tile([P, hi - lo], U8, name=f"wo_scales{load}", align_bytes=64)
             nc.vector.quantize_mx(
-                out=wo_codes[:].bitcast(E4M3), scales=wo_scales[:], in_=wo_words[:].rearrange("p c t -> p (c t)")
+                out=wo_codes[:].bitcast(E4M3), scales=wo_scales[:], in_=wo_words.rearrange("p c t -> p (c t)")
             )
             for k in range(0, hi - lo, P):
                 stationary.append((wo_codes[:, k : k + P], wo_scales[:, k : k + P]))
@@ -150,9 +150,18 @@ def tile_attend_gdelta_kernel(tc, dyT, oT, wo, gq, offs, out_0, out_1):
         quantize_dy(0, HALF)
         quantize_wo(0, first_words)
         early_bank = product(0, 0, "ring0")
-        nc.vector.tensor_copy(dy_words[:, HALF:N, 1], dy_planes[3][:].indirect(lists[1]))
-        quantize_wo(1, lay_out_wo(1, nc.scalar.copy))
-        quantize_dy(HALF, HALF)
+        second = keep.tile([P, P * PACK + HALF], BF16, name="second", tag="raw0", align_bytes=64)
+        second_words = second[:, 0 : P * PACK].rearrange("p (c t) -> p c t", t=PACK)
+        last_row = second[:, P * PACK :]
+        weave(nc.scalar.copy, second_words, wo_raw[1][:])
+        for c, copy in ((3, nc.scalar.copy), (2, nc.vector.tensor_copy)):
+            piece = last_row[:, (c - 2) * P : (c - 1) * P]
+            nc.vector.tensor_copy(piece, dy_planes[3][:].indirect(offsets[:, c * P // 16 : (c + 1) * P // 16]))
+        quantize_wo(1, second_words)
+        for c, copy in ((3, nc.scalar.copy), (2, nc.vector.tensor_copy)):
+            copy(dy_words[:, c * P : (c + 1) * P, 1], last_row[:, (c - 2) * P : (c - 1) * P])
+        for c in (3, 2):
+            quantize_dy(c * P, P)
         b = [keep.tile([P, N], F32, name=f"b{j}") for j in range(TILES)]
         nc.scalar.copy(b[0][:, 0:HALF], early_bank[:, HALF:N])
         nc.vector.tensor_tensor(windows[0][:].indirect(lists[0]), b[0][:, 0:HALF], gate[:, 0:HALF], MULT)

@@ -20,18 +20,17 @@ COPY = mybir.ActivationFunctionType.Copy
 
 P = 128
 PACK = 4
+BAND = 16
 TILES = E // P
 BLOCKS = N // P
+HALF = N // 2
 RUN = T // P
 LINE = 4
 QUADRANT = 32
-WINDOWS = 3
-WO_LOADS = [(0, 128), (128, 256), (256, 512)]
-WORDS_TAGS = ("early", "raw0", "gates")
 PLACES = (2, 3, 0, 1)
-WINDOW_OF = (0, 1, 2, 0)
-BANK_OF = ("ring1", "ring0", "ring1", "ring0")
-HALF = N // 2
+WO_LOADS = [(0, 128), (128, 256), (256, 512)]
+WINDOWS = 3
+RING = ("ring0", "ring1")
 
 
 def tile_attend_gdelta_kernel(tc, dyT, oT, wo, gq, offs, out_0, out_1):
@@ -41,24 +40,32 @@ def tile_attend_gdelta_kernel(tc, dyT, oT, wo, gq, offs, out_0, out_1):
         psum = ctx.enter_context(tc.psum_pool(name="psum", bufs=1))
         psum_b = ctx.enter_context(tc.psum_pool(name="psum_b", bufs=1))
 
-        offsets = keep.tile([P, N // 16], U16, name="offsets")
-        dy_planes = [keep.tile([P, T], F32, name=f"dy{t}") for t in range(PACK)]
+        offsets = keep.tile([P, N // BAND], U16, name="offsets")
+        dy_planes = [keep.tile([P, T], F32, name=f"dy{k}") for k in range(PACK)]
         o_tiles = [keep.tile([P, T], F32, name=f"o{j}") for j in range(TILES)]
-        wo_raw = [keep.tile([P, PACK, hi - lo], F32, name=f"wo_raw{lo}", tag=f"raw{lo}", align_bytes=64) for lo, hi in WO_LOADS]
+        wo_raw = [
+            keep.tile([P, PACK, hi - lo], F32, name=f"wo_raw{lo}", tag=f"raw{lo}", align_bytes=64)
+            for lo, hi in WO_LOADS
+        ]
         dy_rows = dyT.rearrange("(p t) n -> t p n", t=PACK)
 
         gate_runs = keep.tile([P, RUN], F32, name="gate_runs")
         nc.scalar.dma_start(gate_runs[:], gq[0:1, :].rearrange("o (p u) -> (o p) u", u=RUN))
         nc.sync.dma_start(dy_planes[0][:], dy_rows[PLACES[0]])
         nc.sync.dma_start(offsets[:], offs)
-        for t in range(1, PACK):
-            nc.sync.dma_start(dy_planes[t][:], dy_rows[PLACES[t]])
+        for k in range(1, PACK):
+            nc.sync.dma_start(dy_planes[k][:], dy_rows[PLACES[k]])
         for raw, (lo, hi) in zip(wo_raw, WO_LOADS):
             nc.sync.dma_start(raw[:], wo[:, lo:hi].rearrange("(p t) c -> p t c", t=PACK))
         for j in range(TILES):
             nc.sync.dma_start(o_tiles[j][:], oT[j * P : (j + 1) * P, :])
 
-        windows = [keep.tile([P, T], F32, name=f"window{w}", tag=f"window{w}", align_bytes=64) for w in range(WINDOWS)]
+        def listed(window, lo, hi):
+            return window[:].indirect(offsets[:, lo // BAND : hi // BAND])
+
+        windows = [
+            keep.tile([P, T], F32, name=f"window{w}", tag=f"window{w}", align_bytes=64) for w in range(WINDOWS)
+        ]
         nc.vector.memset(windows[0][:], 0.0)
         identity = keep.tile([P, P], F32, name="identity")
         make_identity(nc, identity[:])
@@ -85,21 +92,21 @@ def tile_attend_gdelta_kernel(tc, dyT, oT, wo, gq, offs, out_0, out_1):
                 spread[:].rearrange("p u k -> p k u"),
                 COPY,
             )
-
         gate = keep.tile([P, N], F32, name="gate")
-        nc.vector.tensor_copy(gate[:], gate_window[:].indirect(offsets[:]))
-        lists = [offsets[:, 0 : HALF // 16], offsets[:, HALF // 16 : N // 16]]
+        nc.vector.tensor_copy(gate[:], listed(gate_window, 0, N))
+
+        last_block = (BLOCKS - 1) * P
         staged = keep.tile([P, N * PACK + P], BF16, name="staged", tag="gates", align_bytes=64)
         dy_words = staged[:, 0 : N * PACK].rearrange("p (n t) -> p n t", t=PACK)
         third_row = staged[:, N * PACK :]
         dy_early = keep.tile([P, 2, N], BF16, name="dy_early", tag="early", align_bytes=64)
-        for t in range(2):
-            nc.vector.tensor_copy(dy_early[:, t, :], dy_planes[t][:].indirect(offsets[:]))
+        for k in range(2):
+            nc.vector.tensor_copy(dy_early[:, k, :], listed(dy_planes[k], 0, N))
         nc.scalar.copy(dy_words[:, :, 2:4], dy_early[:].rearrange("p t n -> p n t"))
-        nc.vector.tensor_copy(third_row, dy_planes[2][:].indirect(offsets[:, 3 * P // 16 :]))
-        nc.scalar.copy(dy_words[:, 3 * P :, 0], third_row)
-        nc.vector.tensor_copy(dy_words[:, 0 : 3 * P, 0], dy_planes[2][:].indirect(offsets[:, 0 : 3 * P // 16]))
-        nc.vector.tensor_copy(dy_words[:, 0:HALF, 1], dy_planes[3][:].indirect(lists[0]))
+        nc.vector.tensor_copy(third_row, listed(dy_planes[2], last_block, N))
+        nc.scalar.copy(dy_words[:, last_block:, 0], third_row)
+        nc.vector.tensor_copy(dy_words[:, 0:last_block, 0], listed(dy_planes[2], 0, last_block))
+        nc.vector.tensor_copy(dy_words[:, 0:HALF, 1], listed(dy_planes[3], 0, HALF))
 
         def weave(copy, words, rows):
             copy(
@@ -116,15 +123,9 @@ def tile_attend_gdelta_kernel(tc, dyT, oT, wo, gq, offs, out_0, out_1):
 
         stationary = []
 
-        def lay_out_wo(load, copy):
-            lo, hi = WO_LOADS[load]
-            wo_words = keep.tile([P, hi - lo, PACK], BF16, name=f"wo_words{load}", tag=WORDS_TAGS[load], align_bytes=64)
-            weave(copy, wo_words[:], wo_raw[load][:])
-            return wo_words[:]
-
         def quantize_wo(load, wo_words):
             lo, hi = WO_LOADS[load]
-            wo_codes = keep.tile([P, hi - lo], U32, name=f"wo_codes{load}", tag=f"codes{load}", align_bytes=64)
+            wo_codes = keep.tile([P, hi - lo], U32, name=f"wo_codes{load}", align_bytes=64)
             wo_scales = keep.tile([P, hi - lo], U8, name=f"wo_scales{load}", align_bytes=64)
             nc.vector.quantize_mx(
                 out=wo_codes[:].bitcast(E4M3), scales=wo_scales[:], in_=wo_words.rearrange("p c t -> p (c t)")
@@ -132,89 +133,91 @@ def tile_attend_gdelta_kernel(tc, dyT, oT, wo, gq, offs, out_0, out_1):
             for k in range(0, hi - lo, P):
                 stationary.append((wo_codes[:, k : k + P], wo_scales[:, k : k + P]))
 
-        def product(j, lo, tag):
+        def product(j, first_column, tag):
             wo_codes, wo_scales = stationary[j]
             bank = psum_b.tile([P, N], F32, name="bank", tag=tag)
             nc.tensor.matmul_mx(
                 out=bank[:],
                 lhsT=wo_codes.bitcast(E4M3),
                 lhsT_scale=wo_scales,
-                rhs=dy_codes[:, lo : lo + N].bitcast(E5M2),
-                rhs_scale=dy_scales[:, lo : lo + N],
+                rhs=dy_codes[:, first_column : first_column + N].bitcast(E5M2),
+                rhs_scale=dy_scales[:, first_column : first_column + N],
                 start=True,
                 stop=True,
             )
             return bank
 
-        first_words = lay_out_wo(0, nc.vector.tensor_copy)
+        first_flat = keep.tile([P, P * PACK], BF16, name="first_flat", tag="early", align_bytes=64)
+        first_words = first_flat[:].rearrange("p (c t) -> p c t", t=PACK)
+        for lo, copy in ((0, nc.vector.tensor_copy), (P // 2, nc.scalar.copy)):
+            weave(copy, first_words[:, lo : lo + P // 2, :], wo_raw[0][:, :, lo : lo + P // 2])
         quantize_dy(0, HALF)
         quantize_wo(0, first_words)
-        early_bank = product(0, 0, "ring0")
+        early_bank = product(0, 0, RING[0])
+
         second = keep.tile([P, P * PACK + HALF], BF16, name="second", tag="raw0", align_bytes=64)
         second_words = second[:, 0 : P * PACK].rearrange("p (c t) -> p c t", t=PACK)
         last_row = second[:, P * PACK :]
         weave(nc.scalar.copy, second_words, wo_raw[1][:])
-        for c, copy in ((3, nc.scalar.copy), (2, nc.vector.tensor_copy)):
-            piece = last_row[:, (c - 2) * P : (c - 1) * P]
-            nc.vector.tensor_copy(piece, dy_planes[3][:].indirect(offsets[:, c * P // 16 : (c + 1) * P // 16]))
+        late_blocks = ((last_block, nc.scalar.copy), (HALF, nc.vector.tensor_copy))
+        for lo, copy in late_blocks:
+            nc.vector.tensor_copy(last_row[:, lo - HALF : lo - HALF + P], listed(dy_planes[3], lo, lo + P))
         quantize_wo(1, second_words)
-        for c, copy in ((3, nc.scalar.copy), (2, nc.vector.tensor_copy)):
-            copy(dy_words[:, c * P : (c + 1) * P, 1], last_row[:, (c - 2) * P : (c - 1) * P])
-        for c in (3, 2):
-            quantize_dy(c * P, P)
+        for lo, copy in late_blocks:
+            copy(dy_words[:, lo : lo + P, 1], last_row[:, lo - HALF : lo - HALF + P])
+        for lo, copy in late_blocks:
+            quantize_dy(lo, P)
+
         b = [keep.tile([P, N], F32, name=f"b{j}") for j in range(TILES)]
         nc.scalar.copy(b[0][:, 0:HALF], early_bank[:, HALF:N])
-        nc.vector.tensor_tensor(windows[0][:].indirect(lists[0]), b[0][:, 0:HALF], gate[:, 0:HALF], MULT)
-        quantize_wo(2, lay_out_wo(2, nc.scalar.copy))
+        nc.vector.tensor_tensor(listed(windows[0], 0, HALF), b[0][:, 0:HALF], gate[:, 0:HALF], MULT)
+
+        rest_words = keep.tile([P, 2 * P, PACK], BF16, name="wo_words2", tag="gates", align_bytes=64)
+        weave(nc.scalar.copy, rest_words[:], wo_raw[2][:])
+        quantize_wo(2, rest_words[:])
 
         gate_cols = keep.tile([P, BLOCKS], F32, name="gate_cols")
 
         def turn_gates():
-            turned = psum_b.tile([P, BLOCKS, P], F32, name="turned", tag="ring0")
+            turned = psum_b.tile([P, BLOCKS, P], F32, name="turned", tag=RING[0])
             for c in range(BLOCKS):
                 nc.tensor.transpose(turned[:, c, :], gate[:, c * P : (c + 1) * P], identity[:])
             nc.scalar.copy(gate_cols[:], turned[:, :, 0])
 
         sums = [psum.tile([P, P], F32, name=f"sums{c}", tag=f"bank{c}") for c in range(BLOCKS)]
 
-        def product_and_scatter(j):
-            bank = product(j, HALF, BANK_OF[j])
-            window = windows[WINDOW_OF[j]]
-            lo = HALF if j == 0 else 0
+        def product_and_scatter(j, lo):
+            bank = product(j, HALF, RING[(j + 1) % 2])
+            window = windows[j % WINDOWS]
             nc.scalar.copy(b[j][:, lo:], bank[:, lo:])
-            nc.vector.tensor_tensor(window[:].indirect(offsets[:, lo // 16 :]), b[j][:, lo:], gate[:, lo:], MULT)
+            nc.vector.tensor_tensor(listed(window, lo, N), b[j][:, lo:], gate[:, lo:], MULT)
             nc.sync.dma_start(out_0[j * P : (j + 1) * P, :], window[:])
 
-        def add_to_delta(j, first, last, q):
-            nc.vector.tensor_tensor(
-                q,
-                o_tiles[j][:].indirect(offsets[:, first * P // 16 : last * P // 16]),
-                b[j][:, first * P : last * P],
-                MULT,
-            )
-            for c in range(first, last):
+        def add_to_delta(j, lo, hi, q):
+            nc.vector.tensor_tensor(q, listed(o_tiles[j], lo, hi), b[j][:, lo:hi], MULT)
+            for first in range(lo, hi, P):
                 nc.tensor.matmul(
-                    sums[c][:],
-                    q[:, (c - first) * P : (c - first + 1) * P],
+                    sums[first // P][:],
+                    q[:, first - lo : first - lo + P],
                     identity[:],
                     start=(j == 0),
                     stop=(j == TILES - 1),
                     is_transpose=True,
                 )
 
-        product_and_scatter(0)
-        product_and_scatter(1)
+        product_and_scatter(0, HALF)
+        product_and_scatter(1, 0)
         turn_gates()
-        add_to_delta(0, 0, BLOCKS, keep.tile([P, N], F32, name="q0")[:])
-        add_to_delta(1, 0, BLOCKS, keep.tile([P, N], F32, name="q1")[:])
-        product_and_scatter(2)
-        add_to_delta(2, 0, BLOCKS, keep.tile([P, N], F32, name="q2")[:])
-        product_and_scatter(3)
-        add_to_delta(3, 0, 2, keep.tile([P, N // 2], F32, name="q3")[:])
-        late = keep.tile([P, N // 2 + QUADRANT], F32, name="late", tag="window1", align_bytes=64)
-        add_to_delta(3, 2, BLOCKS, late[:, 0 : N // 2])
+        add_to_delta(0, 0, N, keep.tile([P, N], F32, name="q0")[:])
+        add_to_delta(1, 0, N, keep.tile([P, N], F32, name="q1")[:])
+        product_and_scatter(2, 0)
+        add_to_delta(2, 0, N, keep.tile([P, N], F32, name="q2")[:])
+        product_and_scatter(3, 0)
+        add_to_delta(3, 0, HALF, keep.tile([P, HALF], F32, name="q3")[:])
+        late = keep.tile([P, HALF + QUADRANT], F32, name="late", tag="window1", align_bytes=64)
+        add_to_delta(3, HALF, N, late[:, 0:HALF])
         last_rows = keep.tile([P, QUADRANT], F32, name="last_rows", align_bytes=64)
-        rows = [late[:, N // 2 :], last_rows[:]]
+        row_tiles = [late[:, HALF:], last_rows[:]]
 
         gated = keep.tile([P, BLOCKS, P], F32, name="gated")
         for h in range(2):
@@ -222,12 +225,14 @@ def tile_attend_gdelta_kernel(tc, dyT, oT, wo, gq, offs, out_0, out_1):
                 c = 2 * h + k
                 column = delta_cols[h][:, k : k + 1]
                 if c < BLOCKS - 1:
-                    nc.scalar.activation(gated[:, c, :], sums[c][:], COPY, scale=gate_cols[:, c : c + 1], accum_out=column)
+                    nc.scalar.activation(
+                        gated[:, c, :], sums[c][:], COPY, scale=gate_cols[:, c : c + 1], accum_out=column
+                    )
                 else:
                     nc.vector.tensor_scalar(
                         gated[:, c, :], sums[c][:], gate_cols[:, c : c + 1], None, MULT, ADD, accum_out=column
                     )
-            delta_rows = rows[h]
+            delta_rows = row_tiles[h]
             nc.vector.transpose(delta_rows, delta_cols[h][:])
             for k, queue in enumerate((nc.scalar if h else nc.sync, nc.sync)):
                 c = 2 * h + k

@@ -17,6 +17,7 @@ E5M2 = mybir.dt.float8_e5m2_x4
 MULT = mybir.AluOpType.mult
 ADD = mybir.AluOpType.add
 COPY = mybir.ActivationFunctionType.Copy
+AXIS_X = mybir.AxisListType.X
 
 P = 128
 PACK = 4
@@ -27,10 +28,7 @@ HALF = N // 2
 RUN = T // P
 LINE = 4
 QUADRANT = 32
-PLACES = (2, 3, 0, 1)
-WO_LOADS = [(0, 128), (128, 256), (256, 512)]
-WINDOWS = 3
-RING = ("ring0", "ring1")
+SPLIT = 384
 
 
 def tile_attend_gdelta_kernel(tc, dyT, oT, wo, gq, offs, out_0, out_1):
@@ -38,48 +36,39 @@ def tile_attend_gdelta_kernel(tc, dyT, oT, wo, gq, offs, out_0, out_1):
     with ExitStack() as ctx:
         keep = ctx.enter_context(tc.tile_pool(name="keep", bufs=1))
         psum = ctx.enter_context(tc.psum_pool(name="psum", bufs=1))
-        psum_b = ctx.enter_context(tc.psum_pool(name="psum_b", bufs=1))
 
         offsets = keep.tile([P, N // BAND], U16, name="offsets")
-        dy_planes = [keep.tile([P, T], F32, name=f"dy{k}") for k in range(PACK)]
+        dy_planes = [keep.tile([P, T], F32, name=f"dy{t}") for t in range(PACK)]
         o_tiles = [keep.tile([P, T], F32, name=f"o{j}") for j in range(TILES)]
-        wo_raw = [
-            keep.tile([P, PACK, hi - lo], F32, name=f"wo_raw{lo}", tag=f"raw{lo}", align_bytes=64)
-            for lo, hi in WO_LOADS
-        ]
+        wo_raw = keep.tile([P, PACK, E], F32, name="wo_raw", align_bytes=64)
         dy_rows = dyT.rearrange("(p t) n -> t p n", t=PACK)
 
-        gate_runs = keep.tile([P, RUN], F32, name="gate_runs")
+        gate_runs = keep.tile([P, RUN], F32, name="gate_runs", tag="gathered1", align_bytes=64)
         nc.scalar.dma_start(gate_runs[:], gq[0:1, :].rearrange("o (p u) -> (o p) u", u=RUN))
-        nc.sync.dma_start(dy_planes[0][:], dy_rows[PLACES[0]])
+        nc.sync.dma_start(dy_planes[0][:], dy_rows[0])
         nc.sync.dma_start(offsets[:], offs)
-        for k in range(1, PACK):
-            nc.sync.dma_start(dy_planes[k][:], dy_rows[PLACES[k]])
-        for raw, (lo, hi) in zip(wo_raw, WO_LOADS):
-            nc.sync.dma_start(raw[:], wo[:, lo:hi].rearrange("(p t) c -> p t c", t=PACK))
+        for t in range(1, PACK):
+            nc.sync.dma_start(dy_planes[t][:], dy_rows[t])
+        nc.sync.dma_start(wo_raw[:], wo.rearrange("(p t) c -> p t c", t=PACK))
         for j in range(TILES):
             nc.sync.dma_start(o_tiles[j][:], oT[j * P : (j + 1) * P, :])
 
         def listed(window, lo, hi):
             return window[:].indirect(offsets[:, lo // BAND : hi // BAND])
 
-        windows = [
-            keep.tile([P, T], F32, name=f"window{w}", tag=f"window{w}", align_bytes=64) for w in range(WINDOWS)
-        ]
+        windows = [keep.tile([P, T], F32, name=f"window{j}", align_bytes=64) for j in range(TILES)]
         nc.vector.memset(windows[0][:], 0.0)
         identity = keep.tile([P, P], F32, name="identity")
         make_identity(nc, identity[:])
-        nc.vector.memset(windows[1][:], 0.0)
-        delta_cols = [keep.tile([P, QUADRANT], F32, name=f"delta_cols{h}", align_bytes=64) for h in range(2)]
-        for cols in delta_cols:
-            nc.gpsimd.memset(cols[:], 0.0)
-        dy_codes = keep.tile([P, HALF + N], U32, name="dy_codes", align_bytes=64)
-        dy_scales = keep.tile([P, HALF + N], U8, name="dy_scales", align_bytes=64)
-        nc.gpsimd.memset(dy_codes[:, 0:HALF], 0)
-        nc.gpsimd.memset(dy_scales[:, 0:HALF], 0)
+        nc.vector.memset(windows[3][:], 0.0)
+        delta_cols = keep.tile([P, BLOCKS, QUADRANT], F32, name="delta_cols", align_bytes=64)
+        nc.gpsimd.memset(delta_cols[:], 0.0)
+        zeros = keep.tile([P, N - SPLIT], F32, name="zeros")
+        nc.gpsimd.memset(zeros[:], 0.0)
+        nc.gpsimd.memset(windows[1][:], 0.0)
         nc.gpsimd.memset(windows[2][:], 0.0)
 
-        gate_window = keep.tile([P, T], F32, name="gate_window", tag="gates", align_bytes=64)
+        gate_window = keep.tile([P, T], F32, name="gate_window", tag="gathered0", align_bytes=64)
         for a in range(RUN // BLOCKS):
             spread = psum.tile([P, BLOCKS, P], F32, name=f"spread{a}", tag=f"bank{a}")
             for u in range(BLOCKS):
@@ -92,151 +81,97 @@ def tile_attend_gdelta_kernel(tc, dyT, oT, wo, gq, offs, out_0, out_1):
                 spread[:].rearrange("p u k -> p k u"),
                 COPY,
             )
-        gate = keep.tile([P, N], F32, name="gate")
+        gate = keep.tile([P, N], F32, name="gate", tag="gate")
         nc.vector.tensor_copy(gate[:], listed(gate_window, 0, N))
 
-        last_block = (BLOCKS - 1) * P
-        staged = keep.tile([P, N * PACK + P], BF16, name="staged", tag="gates", align_bytes=64)
-        dy_words = staged[:, 0 : N * PACK].rearrange("p (n t) -> p n t", t=PACK)
-        third_row = staged[:, N * PACK :]
-        dy_early = keep.tile([P, 2, N], BF16, name="dy_early", tag="early", align_bytes=64)
-        for k in range(2):
-            nc.vector.tensor_copy(dy_early[:, k, :], listed(dy_planes[k], 0, N))
-        nc.scalar.copy(dy_words[:, :, 2:4], dy_early[:].rearrange("p t n -> p n t"))
-        nc.vector.tensor_copy(third_row, listed(dy_planes[2], last_block, N))
-        nc.scalar.copy(dy_words[:, last_block:, 0], third_row)
-        nc.vector.tensor_copy(dy_words[:, 0:last_block, 0], listed(dy_planes[2], 0, last_block))
-        nc.vector.tensor_copy(dy_words[:, 0:HALF, 1], listed(dy_planes[3], 0, HALF))
-
-        def weave(copy, words, rows):
+        gathered = [
+            keep.tile([P, PACK, HALF], BF16, name=f"gathered{h}", tag=f"gathered{h}", align_bytes=64) for h in range(2)
+        ]
+        dy_words = [
+            keep.tile([P, HALF, PACK], BF16, name=f"dy_words{h}", tag=f"words{h}", align_bytes=64) for h in range(2)
+        ]
+        for t in range(PACK):
+            nc.vector.tensor_copy(gathered[0][:, t, :], listed(dy_planes[t], 0, HALF))
+            nc.scalar.activation(gathered[1][:, t, :], listed(dy_planes[t], HALF, N), COPY)
+        for h, copy in enumerate((nc.vector.tensor_copy, nc.scalar.copy)):
             copy(
-                words.rearrange("p (c i) t -> p c t i", i=LINE),
-                rows.rearrange("p t (c i) -> p c t i", i=LINE),
+                dy_words[h][:].rearrange("p (c i) t -> p c t i", i=LINE),
+                gathered[h][:].rearrange("p t (c i) -> p c t i", i=LINE),
             )
-
-        def quantize_dy(lo, count):
+        dy_codes = keep.tile([P, N], U32, name="dy_codes", align_bytes=64)
+        dy_scales = keep.tile([P, N], U8, name="dy_scales", align_bytes=64)
+        for h in range(2):
             nc.vector.quantize_mx(
-                out=dy_codes[:, HALF + lo : HALF + lo + count].bitcast(E5M2),
-                scales=dy_scales[:, HALF + lo : HALF + lo + count],
-                in_=dy_words[:, lo : lo + count, :].rearrange("p n t -> p (n t)"),
+                out=dy_codes[:, h * HALF : (h + 1) * HALF].bitcast(E5M2),
+                scales=dy_scales[:, h * HALF : (h + 1) * HALF],
+                in_=dy_words[h][:].rearrange("p n t -> p (n t)"),
             )
 
-        stationary = []
-
-        def quantize_wo(load, wo_words):
-            lo, hi = WO_LOADS[load]
-            wo_codes = keep.tile([P, hi - lo], U32, name=f"wo_codes{load}", align_bytes=64)
-            wo_scales = keep.tile([P, hi - lo], U8, name=f"wo_scales{load}", align_bytes=64)
+        do = []
+        first_words = keep.tile([P, P * PACK], BF16, name="first_words", tag="words0", align_bytes=64)
+        rest_words = keep.tile([P, (TILES - 1) * P * PACK], BF16, name="rest_words", tag="gathered1", align_bytes=64)
+        for j in range(TILES):
+            flat = first_words[:] if j == 0 else rest_words[:, (j - 1) * P * PACK : j * P * PACK]
+            copy = nc.vector.tensor_copy if j == 0 else nc.scalar.copy
+            copy(
+                flat.rearrange("p (c i t) -> p c t i", i=LINE, t=PACK),
+                wo_raw[:, :, j * P : (j + 1) * P].rearrange("p t (c i) -> p c t i", i=LINE),
+            )
+            wo_codes = keep.tile([P, P], U32, name=f"wo_codes{j}", align_bytes=64)
+            wo_scales = keep.tile([P, P], U8, name=f"wo_scales{j}", align_bytes=64)
             nc.vector.quantize_mx(
-                out=wo_codes[:].bitcast(E4M3), scales=wo_scales[:], in_=wo_words.rearrange("p c t -> p (c t)")
+                out=wo_codes[:].bitcast(E4M3), scales=wo_scales[:], in_=flat
             )
-            for k in range(0, hi - lo, P):
-                stationary.append((wo_codes[:, k : k + P], wo_scales[:, k : k + P]))
-
-        def product(j, first_column, tag):
-            wo_codes, wo_scales = stationary[j]
-            bank = psum_b.tile([P, N], F32, name="bank", tag=tag)
+            bank = psum.tile([P, N], F32, name=f"product{j}")
             nc.tensor.matmul_mx(
                 out=bank[:],
-                lhsT=wo_codes.bitcast(E4M3),
-                lhsT_scale=wo_scales,
-                rhs=dy_codes[:, first_column : first_column + N].bitcast(E5M2),
-                rhs_scale=dy_scales[:, first_column : first_column + N],
+                lhsT=wo_codes[:].bitcast(E4M3),
+                lhsT_scale=wo_scales[:],
+                rhs=dy_codes[:].bitcast(E5M2),
+                rhs_scale=dy_scales[:],
                 start=True,
                 stop=True,
             )
-            return bank
+            gated = keep.tile([P, N], F32, name=f"do{j}")
+            nc.vector.tensor_tensor(gated[:], bank[:], gate[:], MULT)
+            do.append(gated)
 
-        first_flat = keep.tile([P, P * PACK], BF16, name="first_flat", tag="early", align_bytes=64)
-        first_words = first_flat[:].rearrange("p (c t) -> p c t", t=PACK)
-        for lo, copy in ((0, nc.vector.tensor_copy), (P // 2, nc.scalar.copy)):
-            weave(copy, first_words[:, lo : lo + P // 2, :], wo_raw[0][:, :, lo : lo + P // 2])
-        quantize_dy(0, HALF)
-        quantize_wo(0, first_words)
-        early_bank = product(0, 0, RING[0])
+        def store(j):
+            nc.sync.dma_start(out_0[j * P : (j + 1) * P, :], windows[j][:])
 
-        second = keep.tile([P, P * PACK + HALF], BF16, name="second", tag="raw0", align_bytes=64)
-        second_words = second[:, 0 : P * PACK].rearrange("p (c t) -> p c t", t=PACK)
-        last_row = second[:, P * PACK :]
-        weave(nc.scalar.copy, second_words, wo_raw[1][:])
-        late_blocks = ((last_block, nc.scalar.copy), (HALF, nc.vector.tensor_copy))
-        for lo, copy in late_blocks:
-            nc.vector.tensor_copy(last_row[:, lo - HALF : lo - HALF + P], listed(dy_planes[3], lo, lo + P))
-        quantize_wo(1, second_words)
-        for lo, copy in late_blocks:
-            copy(dy_words[:, lo : lo + P, 1], last_row[:, lo - HALF : lo - HALF + P])
-        for lo, copy in late_blocks:
-            quantize_dy(lo, P)
+        def scatter_on_scalar(j):
+            nc.scalar.activation(listed(windows[j], 0, SPLIT), do[j][:, 0:SPLIT], COPY)
 
-        b = [keep.tile([P, N], F32, name=f"b{j}") for j in range(TILES)]
-        nc.scalar.copy(b[0][:, 0:HALF], early_bank[:, HALF:N])
-        nc.vector.tensor_tensor(listed(windows[0], 0, HALF), b[0][:, 0:HALF], gate[:, 0:HALF], MULT)
+        def scatter_on_vector(j):
+            nc.vector.tensor_tensor(listed(windows[j], SPLIT, N), do[j][:, SPLIT:], zeros[:], ADD)
 
-        rest_words = keep.tile([P, 2 * P, PACK], BF16, name="wo_words2", tag="gates", align_bytes=64)
-        weave(nc.scalar.copy, rest_words[:], wo_raw[2][:])
-        quantize_wo(2, rest_words[:])
-
-        gate_cols = keep.tile([P, BLOCKS], F32, name="gate_cols")
-
-        def turn_gates():
-            turned = psum_b.tile([P, BLOCKS, P], F32, name="turned", tag=RING[0])
-            for c in range(BLOCKS):
-                nc.tensor.transpose(turned[:, c, :], gate[:, c * P : (c + 1) * P], identity[:])
-            nc.scalar.copy(gate_cols[:], turned[:, :, 0])
+        for j in range(TILES):
+            for scatter in (scatter_on_scalar, scatter_on_vector) if j == 0 else (scatter_on_vector, scatter_on_scalar):
+                scatter(j)
+            store(j)
 
         sums = [psum.tile([P, P], F32, name=f"sums{c}", tag=f"bank{c}") for c in range(BLOCKS)]
-
-        def product_and_scatter(j, lo):
-            bank = product(j, HALF, RING[(j + 1) % 2])
-            window = windows[j % WINDOWS]
-            nc.scalar.copy(b[j][:, lo:], bank[:, lo:])
-            nc.vector.tensor_tensor(listed(window, lo, N), b[j][:, lo:], gate[:, lo:], MULT)
-            nc.sync.dma_start(out_0[j * P : (j + 1) * P, :], window[:])
-
-        def add_to_delta(j, lo, hi, q):
-            nc.vector.tensor_tensor(q, listed(o_tiles[j], lo, hi), b[j][:, lo:hi], MULT)
-            for first in range(lo, hi, P):
+        q_all = keep.tile([P, TILES * N], F32, name="q_all", tag="gate")
+        for j in range(TILES):
+            q = q_all[:, j * N : (j + 1) * N]
+            nc.vector.tensor_tensor(q, listed(o_tiles[j], 0, N), do[j][:], MULT)
+            for c in range(BLOCKS):
                 nc.tensor.matmul(
-                    sums[first // P][:],
-                    q[:, first - lo : first - lo + P],
+                    sums[c][:],
+                    q[:, c * P : (c + 1) * P],
                     identity[:],
                     start=(j == 0),
                     stop=(j == TILES - 1),
                     is_transpose=True,
                 )
 
-        product_and_scatter(0, HALF)
-        product_and_scatter(1, 0)
-        turn_gates()
-        add_to_delta(0, 0, N, keep.tile([P, N], F32, name="q0")[:])
-        add_to_delta(1, 0, N, keep.tile([P, N], F32, name="q1")[:])
-        product_and_scatter(2, 0)
-        add_to_delta(2, 0, N, keep.tile([P, N], F32, name="q2")[:])
-        product_and_scatter(3, 0)
-        add_to_delta(3, 0, HALF, keep.tile([P, HALF], F32, name="q3")[:])
-        late = keep.tile([P, HALF + QUADRANT], F32, name="late", tag="window1", align_bytes=64)
-        add_to_delta(3, HALF, N, late[:, 0:HALF])
-        last_rows = keep.tile([P, QUADRANT], F32, name="last_rows", align_bytes=64)
-        row_tiles = [late[:, HALF:], last_rows[:]]
-
-        gated = keep.tile([P, BLOCKS, P], F32, name="gated")
-        for h in range(2):
-            for k in range(2):
-                c = 2 * h + k
-                column = delta_cols[h][:, k : k + 1]
-                if c < BLOCKS - 1:
-                    nc.scalar.activation(
-                        gated[:, c, :], sums[c][:], COPY, scale=gate_cols[:, c : c + 1], accum_out=column
-                    )
-                else:
-                    nc.vector.tensor_scalar(
-                        gated[:, c, :], sums[c][:], gate_cols[:, c : c + 1], None, MULT, ADD, accum_out=column
-                    )
-            delta_rows = row_tiles[h]
-            nc.vector.transpose(delta_rows, delta_cols[h][:])
-            for k, queue in enumerate((nc.scalar if h else nc.sync, nc.sync)):
-                c = 2 * h + k
-                queue.dma_start(
-                    out_1[:, c * P : (c + 1) * P].rearrange("o (q r) -> (o q) r", r=QUADRANT),
-                    delta_rows[k : P : QUADRANT, :],
-                )
+        for c in range(BLOCKS):
+            nc.vector.tensor_reduce(delta_cols[:, c, 0:1], sums[c][:], AXIS_X, ADD)
+        delta_rows = keep.tile([P, BLOCKS, QUADRANT], F32, name="delta_rows", align_bytes=64)
+        nc.vector.transpose(
+            delta_rows[:].rearrange("p c k -> p (c k)"), delta_cols[:].rearrange("p c k -> p (c k)")
+        )
+        nc.scalar.dma_start(
+            out_1.rearrange("o (c r k) -> (o r) c k", c=BLOCKS, k=QUADRANT),
+            delta_rows[0:P:QUADRANT, :, :],
+        )

@@ -28,7 +28,7 @@ HALF = N // 2
 RUN = T // P
 LINE = 4
 QUADRANT = 32
-SPLIT = 384
+SPLIT = 320
 
 
 def tile_attend_gdelta_kernel(tc, dyT, oT, wo, gq, offs, out_0, out_1):
@@ -93,11 +93,15 @@ def tile_attend_gdelta_kernel(tc, dyT, oT, wo, gq, offs, out_0, out_1):
         for t in range(PACK):
             nc.vector.tensor_copy(gathered[0][:, t, :], listed(dy_planes[t], 0, HALF))
             nc.scalar.activation(gathered[1][:, t, :], listed(dy_planes[t], HALF, N), COPY)
-        for h, copy in enumerate((nc.vector.tensor_copy, nc.scalar.copy)):
+        def weave(copy, words, rows):
             copy(
-                dy_words[h][:].rearrange("p (c i) t -> p c t i", i=LINE),
-                gathered[h][:].rearrange("p t (c i) -> p c t i", i=LINE),
+                words.rearrange("p (c i) t -> p c t i", i=LINE),
+                rows.rearrange("p t (c i) -> p c t i", i=LINE),
             )
+
+        weave(nc.vector.tensor_copy, dy_words[0][:], gathered[0][:])
+        weave(nc.vector.tensor_copy, dy_words[1][:, 0:P, :], gathered[1][:, :, 0:P])
+        weave(nc.scalar.copy, dy_words[1][:, P:, :], gathered[1][:, :, P:])
         dy_codes = keep.tile([P, N], U32, name="dy_codes", align_bytes=64)
         dy_scales = keep.tile([P, N], U8, name="dy_scales", align_bytes=64)
         for h in range(2):
@@ -107,66 +111,80 @@ def tile_attend_gdelta_kernel(tc, dyT, oT, wo, gq, offs, out_0, out_1):
                 in_=dy_words[h][:].rearrange("p n t -> p (n t)"),
             )
 
-        do = []
-        first_words = keep.tile([P, P * PACK], BF16, name="first_words", tag="words0", align_bytes=64)
-        rest_words = keep.tile([P, (TILES - 1) * P * PACK], BF16, name="rest_words", tag="gathered1", align_bytes=64)
-        for j in range(TILES):
-            flat = first_words[:] if j == 0 else rest_words[:, (j - 1) * P * PACK : j * P * PACK]
-            copy = nc.vector.tensor_copy if j == 0 else nc.scalar.copy
-            copy(
-                flat.rearrange("p (c i t) -> p c t i", i=LINE, t=PACK),
-                wo_raw[:, :, j * P : (j + 1) * P].rearrange("p t (c i) -> p c t i", i=LINE),
-            )
-            wo_codes = keep.tile([P, P], U32, name=f"wo_codes{j}", align_bytes=64)
-            wo_scales = keep.tile([P, P], U8, name=f"wo_scales{j}", align_bytes=64)
-            nc.vector.quantize_mx(
-                out=wo_codes[:].bitcast(E4M3), scales=wo_scales[:], in_=flat
-            )
-            bank = psum.tile([P, N], F32, name=f"product{j}")
+        wo_codes = keep.tile([P, E], U32, name="wo_codes", align_bytes=64)
+        wo_scales = keep.tile([P, E], U8, name="wo_scales", align_bytes=64)
+
+        def quantize_wo(copy, flat, lo, hi):
+            weave(copy, flat.rearrange("p (c t) -> p c t", t=PACK), wo_raw[:, :, lo:hi])
+            nc.vector.quantize_mx(out=wo_codes[:, lo:hi].bitcast(E4M3), scales=wo_scales[:, lo:hi], in_=flat)
+
+        do = [keep.tile([P, N], F32, name=f"do{j}") for j in range(TILES)]
+
+        def gated_product(j, lo, hi, tag):
+            bank = psum.tile([P, hi - lo], F32, name="product", tag=tag)
             nc.tensor.matmul_mx(
                 out=bank[:],
-                lhsT=wo_codes[:].bitcast(E4M3),
-                lhsT_scale=wo_scales[:],
-                rhs=dy_codes[:].bitcast(E5M2),
-                rhs_scale=dy_scales[:],
+                lhsT=wo_codes[:, j * P : (j + 1) * P].bitcast(E4M3),
+                lhsT_scale=wo_scales[:, j * P : (j + 1) * P],
+                rhs=dy_codes[:, lo:hi].bitcast(E5M2),
+                rhs_scale=dy_scales[:, lo:hi],
                 start=True,
                 stop=True,
             )
-            gated = keep.tile([P, N], F32, name=f"do{j}")
-            nc.vector.tensor_tensor(gated[:], bank[:], gate[:], MULT)
-            do.append(gated)
+            nc.vector.tensor_tensor(do[j][:, lo:hi], bank[:], gate[:, lo:hi], MULT)
+
+        first_words = keep.tile([P, P * PACK], BF16, name="first_words", tag="words0", align_bytes=64)
+        rest_words = keep.tile([P, (E - P) * PACK], BF16, name="rest_words", tag="gathered1", align_bytes=64)
+        quantize_wo(nc.vector.tensor_copy, first_words[:], 0, P)
+        gated_product(0, 0, HALF, "bank0")
+        gated_product(0, HALF, N, "product0")
+        quantize_wo(nc.scalar.copy, rest_words[:, 0 : P * PACK], P, 2 * P)
+        gated_product(1, 0, N, "product1")
+        quantize_wo(nc.scalar.copy, rest_words[:, P * PACK :], 2 * P, E)
+        gated_product(2, 0, N, "product2")
+        gated_product(3, 0, N, "product3")
 
         def store(j):
             nc.sync.dma_start(out_0[j * P : (j + 1) * P, :], windows[j][:])
 
-        def scatter_on_scalar(j):
-            nc.scalar.activation(listed(windows[j], 0, SPLIT), do[j][:, 0:SPLIT], COPY)
+        def scatter_on_scalar(j, lo, hi):
+            nc.scalar.activation(listed(windows[j], lo, hi), do[j][:, lo:hi], COPY)
 
-        def scatter_on_vector(j):
+        scatter_on_scalar(0, 0, HALF)
+        scatter_on_scalar(0, HALF, N)
+        store(0)
+        for j in range(1, TILES):
             nc.vector.tensor_tensor(listed(windows[j], SPLIT, N), do[j][:, SPLIT:], zeros[:], ADD)
-
-        for j in range(TILES):
-            for scatter in (scatter_on_scalar, scatter_on_vector) if j == 0 else (scatter_on_vector, scatter_on_scalar):
-                scatter(j)
+            scatter_on_scalar(j, 0, SPLIT)
             store(j)
 
         sums = [psum.tile([P, P], F32, name=f"sums{c}", tag=f"bank{c}") for c in range(BLOCKS)]
         q_all = keep.tile([P, TILES * N], F32, name="q_all", tag="gate")
-        for j in range(TILES):
-            q = q_all[:, j * N : (j + 1) * N]
-            nc.vector.tensor_tensor(q, listed(o_tiles[j], 0, N), do[j][:], MULT)
-            for c in range(BLOCKS):
+
+        def add_to_delta(j, lo, hi):
+            q = q_all[:, j * N + lo : j * N + hi]
+            nc.vector.tensor_tensor(q, listed(o_tiles[j], lo, hi), do[j][:, lo:hi], MULT)
+            for first in range(lo, hi, P):
                 nc.tensor.matmul(
-                    sums[c][:],
-                    q[:, c * P : (c + 1) * P],
+                    sums[first // P][:],
+                    q[:, first - lo : first - lo + P],
                     identity[:],
                     start=(j == 0),
                     stop=(j == TILES - 1),
                     is_transpose=True,
                 )
 
+        for j in range(TILES - 1):
+            add_to_delta(j, 0, N)
+        add_to_delta(TILES - 1, 0, HALF)
+        add_to_delta(TILES - 1, HALF, N)
+
+        copied = keep.tile([P, 2, P], F32, name="copied")
         for c in range(BLOCKS):
-            nc.vector.tensor_reduce(delta_cols[:, c, 0:1], sums[c][:], AXIS_X, ADD)
+            if c < 2:
+                nc.scalar.activation(copied[:, c, :], sums[c][:], COPY, accum_out=delta_cols[:, c, 0:1])
+            else:
+                nc.vector.tensor_reduce(delta_cols[:, c, 0:1], sums[c][:], AXIS_X, ADD)
         delta_rows = keep.tile([P, BLOCKS, QUADRANT], F32, name="delta_rows", align_bytes=64)
         nc.vector.transpose(
             delta_rows[:].rearrange("p c k -> p (c k)"), delta_cols[:].rearrange("p c k -> p (c k)")

@@ -28,7 +28,7 @@ HALF = N // 2
 RUN = T // P
 LINE = 4
 QUADRANT = 32
-SPLIT = 320
+SPLIT = 352
 
 
 def tile_attend_gdelta_kernel(tc, dyT, oT, wo, gq, offs, out_0, out_1):
@@ -111,12 +111,14 @@ def tile_attend_gdelta_kernel(tc, dyT, oT, wo, gq, offs, out_0, out_1):
                 in_=dy_words[h][:].rearrange("p n t -> p (n t)"),
             )
 
-        wo_codes = keep.tile([P, E], U32, name="wo_codes", align_bytes=64)
         wo_scales = keep.tile([P, E], U8, name="wo_scales", align_bytes=64)
+        stationary = []
 
-        def quantize_wo(copy, flat, lo, hi):
+        def quantize_wo(copy, flat, lo, hi, tag):
+            wo_codes = keep.tile([P, hi - lo], U32, name="wo_codes", tag=tag, align_bytes=64)
             weave(copy, flat.rearrange("p (c t) -> p c t", t=PACK), wo_raw[:, :, lo:hi])
-            nc.vector.quantize_mx(out=wo_codes[:, lo:hi].bitcast(E4M3), scales=wo_scales[:, lo:hi], in_=flat)
+            nc.vector.quantize_mx(out=wo_codes[:].bitcast(E4M3), scales=wo_scales[:, lo:hi], in_=flat)
+            stationary.extend(wo_codes[:, k : k + P] for k in range(0, hi - lo, P))
 
         do = [keep.tile([P, N], F32, name=f"do{j}") for j in range(TILES)]
 
@@ -124,7 +126,7 @@ def tile_attend_gdelta_kernel(tc, dyT, oT, wo, gq, offs, out_0, out_1):
             bank = psum.tile([P, hi - lo], F32, name="product", tag=tag)
             nc.tensor.matmul_mx(
                 out=bank[:],
-                lhsT=wo_codes[:, j * P : (j + 1) * P].bitcast(E4M3),
+                lhsT=stationary[j].bitcast(E4M3),
                 lhsT_scale=wo_scales[:, j * P : (j + 1) * P],
                 rhs=dy_codes[:, lo:hi].bitcast(E5M2),
                 rhs_scale=dy_scales[:, lo:hi],
@@ -135,12 +137,12 @@ def tile_attend_gdelta_kernel(tc, dyT, oT, wo, gq, offs, out_0, out_1):
 
         first_words = keep.tile([P, P * PACK], BF16, name="first_words", tag="words0", align_bytes=64)
         rest_words = keep.tile([P, (E - P) * PACK], BF16, name="rest_words", tag="gathered1", align_bytes=64)
-        quantize_wo(nc.vector.tensor_copy, first_words[:], 0, P)
+        quantize_wo(nc.vector.tensor_copy, first_words[:], 0, P, "codes0")
         gated_product(0, 0, HALF, "bank0")
         gated_product(0, HALF, N, "product0")
-        quantize_wo(nc.scalar.copy, rest_words[:, 0 : P * PACK], P, 2 * P)
+        quantize_wo(nc.scalar.copy, rest_words[:, 0 : P * PACK], P, 2 * P, "words0")
         gated_product(1, 0, N, "product1")
-        quantize_wo(nc.scalar.copy, rest_words[:, P * PACK :], 2 * P, E)
+        quantize_wo(nc.scalar.copy, rest_words[:, P * PACK :], 2 * P, E, "codes0")
         gated_product(2, 0, N, "product2")
         gated_product(3, 0, N, "product3")
 

@@ -136,13 +136,14 @@ def tile_attend_gdelta_kernel(tc, dyT, oT, wo, gq, offs, out_0, out_1):
             nc.vector.tensor_tensor(do[j][:, lo:hi], bank[:], gate[:, lo:hi], MULT)
 
         first_words = keep.tile([P, P * PACK], BF16, name="first_words", tag="words0", align_bytes=64)
-        rest_words = keep.tile([P, (E - P) * PACK], BF16, name="rest_words", tag="gathered1", align_bytes=64)
+        rest_words = keep.tile([P, (E - 2 * P) * PACK], BF16, name="rest_words", tag="gathered1", align_bytes=64)
         quantize_wo(nc.vector.tensor_copy, first_words[:], 0, P, "codes0")
         gated_product(0, 0, HALF, "bank0")
         gated_product(0, HALF, N, "product0")
-        quantize_wo(nc.scalar.copy, rest_words[:, 0 : P * PACK], P, 2 * P, "words0")
+        second_words = keep.tile([P, P * PACK], BF16, name="second_words", tag="words0", align_bytes=64)
+        quantize_wo(nc.vector.tensor_copy, second_words[:], P, 2 * P, "codes1")
         gated_product(1, 0, N, "product1")
-        quantize_wo(nc.scalar.copy, rest_words[:, P * PACK :], 2 * P, E, "codes0")
+        quantize_wo(nc.scalar.copy, rest_words[:], 2 * P, E, "codes1")
         gated_product(2, 0, N, "product2")
         gated_product(3, 0, N, "product3")
 
@@ -161,10 +162,11 @@ def tile_attend_gdelta_kernel(tc, dyT, oT, wo, gq, offs, out_0, out_1):
             store(j)
 
         sums = [psum.tile([P, P], F32, name=f"sums{c}", tag=f"bank{c}") for c in range(BLOCKS)]
-        q_all = keep.tile([P, TILES * N], F32, name="q_all", tag="gate")
+        q_first = keep.tile([P, N], F32, name="q_first")
+        q_rest = keep.tile([P, (TILES - 1) * N], F32, name="q_rest", tag="gate")
 
         def add_to_delta(j, lo, hi):
-            q = q_all[:, j * N + lo : j * N + hi]
+            q = q_first[:, lo:hi] if j == 0 else q_rest[:, (j - 1) * N + lo : (j - 1) * N + hi]
             nc.vector.tensor_tensor(q, listed(o_tiles[j], lo, hi), do[j][:, lo:hi], MULT)
             for first in range(lo, hi, P):
                 nc.tensor.matmul(

@@ -29,6 +29,7 @@ RUN = T // P
 LINE = 4
 QUADRANT = 32
 SPLIT = 352
+BURST = 256
 
 
 def tile_attend_gdelta_kernel(tc, dyT, oT, wo, gq, offs, out_0, out_1):
@@ -38,9 +39,9 @@ def tile_attend_gdelta_kernel(tc, dyT, oT, wo, gq, offs, out_0, out_1):
         psum = ctx.enter_context(tc.psum_pool(name="psum", bufs=1))
 
         offsets = keep.tile([P, N // BAND], U16, name="offsets")
-        dy_planes = [keep.tile([P, T], F32, name=f"dy{t}") for t in range(PACK)]
-        o_tiles = [keep.tile([P, T], F32, name=f"o{j}") for j in range(TILES)]
-        wo_raw = keep.tile([P, PACK, E], F32, name="wo_raw", align_bytes=64)
+        dy_planes = [keep.tile([P, T], F32, name=f"dy{t}", align_bytes=BURST) for t in range(PACK)]
+        o_tiles = [keep.tile([P, T], F32, name=f"o{j}", align_bytes=BURST) for j in range(TILES)]
+        wo_raw = keep.tile([P, PACK, E], F32, name="wo_raw", align_bytes=BURST)
         dy_rows = dyT.rearrange("(p t) n -> t p n", t=PACK)
 
         gate_runs = keep.tile([P, RUN], F32, name="gate_runs", tag="gathered1", align_bytes=64)
@@ -56,7 +57,7 @@ def tile_attend_gdelta_kernel(tc, dyT, oT, wo, gq, offs, out_0, out_1):
         def listed(window, lo, hi):
             return window[:].indirect(offsets[:, lo // BAND : hi // BAND])
 
-        windows = [keep.tile([P, T], F32, name=f"window{j}", align_bytes=64) for j in range(TILES)]
+        windows = [keep.tile([P, T], F32, name=f"window{j}", align_bytes=BURST) for j in range(TILES)]
         nc.vector.memset(windows[0][:], 0.0)
         identity = keep.tile([P, P], F32, name="identity")
         make_identity(nc, identity[:])

@@ -28,7 +28,7 @@ HALF = N // 2
 RUN = T // P
 LINE = 4
 QUADRANT = 32
-SPLIT = 352
+SPLITS = (352, 320, 320)
 BURST = 256
 
 
@@ -64,7 +64,7 @@ def tile_attend_gdelta_kernel(tc, dyT, oT, wo, gq, offs, out_0, out_1):
         nc.vector.memset(windows[3][:], 0.0)
         delta_cols = keep.tile([P, BLOCKS, QUADRANT], F32, name="delta_cols", align_bytes=64)
         nc.gpsimd.memset(delta_cols[:], 0.0)
-        zeros = keep.tile([P, N - SPLIT], F32, name="zeros")
+        zeros = keep.tile([P, N - min(SPLITS)], F32, name="zeros")
         nc.gpsimd.memset(zeros[:], 0.0)
         nc.gpsimd.memset(windows[1][:], 0.0)
         nc.gpsimd.memset(windows[2][:], 0.0)
@@ -105,7 +105,8 @@ def tile_attend_gdelta_kernel(tc, dyT, oT, wo, gq, offs, out_0, out_1):
         weave(nc.scalar.copy, dy_words[1][:, P:, :], gathered[1][:, :, P:])
         dy_codes = keep.tile([P, N], U32, name="dy_codes", align_bytes=64)
         dy_scales = keep.tile([P, N], U8, name="dy_scales", align_bytes=64)
-        for h in range(2):
+
+        def quantize_dy(h):
             nc.vector.quantize_mx(
                 out=dy_codes[:, h * HALF : (h + 1) * HALF].bitcast(E5M2),
                 scales=dy_scales[:, h * HALF : (h + 1) * HALF],
@@ -113,13 +114,19 @@ def tile_attend_gdelta_kernel(tc, dyT, oT, wo, gq, offs, out_0, out_1):
             )
 
         wo_scales = keep.tile([P, E], U8, name="wo_scales", align_bytes=64)
-        stationary = []
+        wo_codes = keep.tile([P, E], U32, name="wo_codes", align_bytes=64)
+        stationary = [wo_codes[:, j * P : (j + 1) * P] for j in range(TILES)]
 
-        def quantize_wo(copy, flat, lo, hi, tag):
-            wo_codes = keep.tile([P, hi - lo], U32, name="wo_codes", tag=tag, align_bytes=64)
-            weave(copy, flat.rearrange("p (c t) -> p c t", t=PACK), wo_raw[:, :, lo:hi])
-            nc.vector.quantize_mx(out=wo_codes[:].bitcast(E4M3), scales=wo_scales[:, lo:hi], in_=flat)
-            stationary.extend(wo_codes[:, k : k + P] for k in range(0, hi - lo, P))
+        def weave_wo(copy, lo, hi):
+            words = wo_words[:, lo * PACK : hi * PACK].rearrange("p (c t) -> p c t", t=PACK)
+            weave(copy, words, wo_raw[:, :, lo:hi])
+
+        def quantize_wo(lo, hi):
+            nc.vector.quantize_mx(
+                out=wo_codes[:, lo:hi].bitcast(E4M3),
+                scales=wo_scales[:, lo:hi],
+                in_=wo_words[:, lo * PACK : hi * PACK],
+            )
 
         do = [keep.tile([P, N], F32, name=f"do{j}") for j in range(TILES)]
 
@@ -136,17 +143,20 @@ def tile_attend_gdelta_kernel(tc, dyT, oT, wo, gq, offs, out_0, out_1):
             )
             nc.vector.tensor_tensor(do[j][:, lo:hi], bank[:], gate[:, lo:hi], MULT)
 
-        first_words = keep.tile([P, P * PACK], BF16, name="first_words", tag="words0", align_bytes=64)
-        rest_words = keep.tile([P, (E - 2 * P) * PACK], BF16, name="rest_words", tag="gathered1", align_bytes=64)
-        quantize_wo(nc.vector.tensor_copy, first_words[:], 0, P, "codes0")
+        quantize_dy(0)
+        wo_words = keep.tile([P, E * PACK], BF16, name="wo_words", tag="gathered0", align_bytes=64)
+        weave_wo(nc.vector.tensor_copy, 0, P // 2)
+        weave_wo(nc.scalar.copy, P // 2, P)
+        quantize_dy(1)
+        quantize_wo(0, P)
+        weave_wo(nc.vector.tensor_copy, P, 2 * P)
+        weave_wo(nc.scalar.copy, 2 * P, E)
+        quantize_wo(P, 2 * P)
+        quantize_wo(2 * P, E)
         gated_product(0, 0, HALF, "bank0")
         gated_product(0, HALF, N, "product0")
-        second_words = keep.tile([P, P * PACK], BF16, name="second_words", tag="words0", align_bytes=64)
-        quantize_wo(nc.vector.tensor_copy, second_words[:], P, 2 * P, "codes1")
-        gated_product(1, 0, N, "product1")
-        quantize_wo(nc.scalar.copy, rest_words[:], 2 * P, E, "codes1")
-        gated_product(2, 0, N, "product2")
-        gated_product(3, 0, N, "product3")
+        for j in range(1, TILES):
+            gated_product(j, 0, N, f"product{j}")
 
         def store(j):
             nc.sync.dma_start(out_0[j * P : (j + 1) * P, :], windows[j][:])
@@ -157,17 +167,16 @@ def tile_attend_gdelta_kernel(tc, dyT, oT, wo, gq, offs, out_0, out_1):
         scatter_on_scalar(0, 0, HALF)
         scatter_on_scalar(0, HALF, N)
         store(0)
-        for j in range(1, TILES):
-            nc.vector.tensor_tensor(listed(windows[j], SPLIT, N), do[j][:, SPLIT:], zeros[:], ADD)
-            scatter_on_scalar(j, 0, SPLIT)
+        for j, split in enumerate(SPLITS, start=1):
+            nc.vector.tensor_tensor(listed(windows[j], split, N), do[j][:, split:], zeros[:, 0 : N - split], ADD)
+            scatter_on_scalar(j, 0, split)
             store(j)
 
         sums = [psum.tile([P, P], F32, name=f"sums{c}", tag=f"bank{c}") for c in range(BLOCKS)]
-        q_first = keep.tile([P, N], F32, name="q_first")
-        q_rest = keep.tile([P, (TILES - 1) * N], F32, name="q_rest", tag="gate")
+        products = keep.tile([P, TILES * N], F32, name="products", tag="gate")
 
         def add_to_delta(j, lo, hi):
-            q = q_first[:, lo:hi] if j == 0 else q_rest[:, (j - 1) * N + lo : (j - 1) * N + hi]
+            q = products[:, j * N + lo : j * N + hi]
             nc.vector.tensor_tensor(q, listed(o_tiles[j], lo, hi), do[j][:, lo:hi], MULT)
             for first in range(lo, hi, P):
                 nc.tensor.matmul(

@@ -38,18 +38,20 @@ def tile_attend_gdelta_kernel(tc, dyT, oT, wo, gq, offs, out_0, out_1):
         keep = ctx.enter_context(tc.tile_pool(name="keep", bufs=1))
         psum = ctx.enter_context(tc.psum_pool(name="psum", bufs=1))
 
-        offsets = keep.tile([P, N // BAND], U16, name="offsets")
-        dy_planes = [keep.tile([P, T], F32, name=f"dy{t}", align_bytes=BURST) for t in range(PACK)]
+        offsets = keep.tile([P, N // BAND], U16, name="offsets", align_bytes=BURST)
+        dy_first = keep.tile([P, T], F32, name="dy_first", align_bytes=BURST)
+        dy_middle = keep.tile([P, 2 * T], F32, name="dy_middle", align_bytes=BURST)
+        dy_last = keep.tile([P, T], F32, name="dy_last", align_bytes=BURST)
         o_tiles = [keep.tile([P, T], F32, name=f"o{j}", align_bytes=BURST) for j in range(TILES)]
         wo_raw = keep.tile([P, PACK, E], F32, name="wo_raw", align_bytes=BURST)
-        dy_rows = dyT.rearrange("(p t) n -> t p n", t=PACK)
+        dy_rows = dyT.rearrange("(p t) n -> p (t n)", t=PACK)
 
-        gate_runs = keep.tile([P, RUN], F32, name="gate_runs", tag="gathered1", align_bytes=64)
+        gate_runs = keep.tile([P, RUN], F32, name="gate_runs", tag="gathered1", align_bytes=BURST)
         nc.scalar.dma_start(gate_runs[:], gq[0:1, :].rearrange("o (p u) -> (o p) u", u=RUN))
-        nc.sync.dma_start(dy_planes[0][:], dy_rows[0])
+        nc.sync.dma_start(dy_first[:], dy_rows[:, 0:T])
         nc.sync.dma_start(offsets[:], offs)
-        for t in range(1, PACK):
-            nc.sync.dma_start(dy_planes[t][:], dy_rows[t])
+        nc.sync.dma_start(dy_middle[:], dy_rows[:, T : 3 * T])
+        nc.sync.dma_start(dy_last[:], dy_rows[:, 3 * T :])
         nc.sync.dma_start(wo_raw[:], wo.rearrange("(p t) c -> p t c", t=PACK))
         for j in range(TILES):
             nc.sync.dma_start(o_tiles[j][:], oT[j * P : (j + 1) * P, :])
@@ -69,7 +71,7 @@ def tile_attend_gdelta_kernel(tc, dyT, oT, wo, gq, offs, out_0, out_1):
         nc.gpsimd.memset(windows[1][:], 0.0)
         nc.gpsimd.memset(windows[2][:], 0.0)
 
-        gate_window = keep.tile([P, T], F32, name="gate_window", tag="gathered0", align_bytes=64)
+        gate_window = keep.tile([P, T], F32, name="gate_window", tag="gathered0", align_bytes=BURST)
         for a in range(RUN // BLOCKS):
             spread = psum.tile([P, BLOCKS, P], F32, name=f"spread{a}", tag=f"bank{a}")
             for u in range(BLOCKS):
@@ -86,23 +88,35 @@ def tile_attend_gdelta_kernel(tc, dyT, oT, wo, gq, offs, out_0, out_1):
         nc.vector.tensor_copy(gate[:], listed(gate_window, 0, N))
 
         gathered = [
-            keep.tile([P, PACK, HALF], BF16, name=f"gathered{h}", tag=f"gathered{h}", align_bytes=64) for h in range(2)
+            keep.tile([P, PACK + 2, HALF], BF16, name=f"gathered{h}", tag=f"gathered{h}", align_bytes=BURST)
+            for h in range(2)
         ]
         dy_words = [
             keep.tile([P, HALF, PACK], BF16, name=f"dy_words{h}", tag=f"words{h}", align_bytes=64) for h in range(2)
         ]
-        for t in range(PACK):
-            nc.vector.tensor_copy(gathered[0][:, t, :], listed(dy_planes[t], 0, HALF))
-            nc.scalar.activation(gathered[1][:, t, :], listed(dy_planes[t], HALF, N), COPY)
+
+        def gather_plane(t, window):
+            nc.vector.tensor_copy(gathered[0][:, t, :], listed(window, 0, HALF))
+            nc.scalar.activation(gathered[1][:, t, :], listed(window, HALF, N), COPY)
+
+        gather_plane(0, dy_first)
+        third = [rows[:, PACK:, :].rearrange("p a n -> p (a n)").bitcast(F32) for rows in gathered]
+        nc.vector.tensor_copy(third[0], listed(dy_middle[:, T:], 0, HALF))
+        nc.scalar.activation(third[1], listed(dy_middle[:, T:], HALF, N), COPY)
+        gather_plane(1, dy_middle)
+        nc.vector.tensor_copy(gathered[0][:, 2, :], third[0])
+        nc.scalar.copy(gathered[1][:, 2, :], third[1])
+        gather_plane(3, dy_last)
+
         def weave(copy, words, rows):
             copy(
                 words.rearrange("p (c i) t -> p c t i", i=LINE),
                 rows.rearrange("p t (c i) -> p c t i", i=LINE),
             )
 
-        weave(nc.vector.tensor_copy, dy_words[0][:], gathered[0][:])
-        weave(nc.vector.tensor_copy, dy_words[1][:, 0:P, :], gathered[1][:, :, 0:P])
-        weave(nc.scalar.copy, dy_words[1][:, P:, :], gathered[1][:, :, P:])
+        weave(nc.vector.tensor_copy, dy_words[0][:], gathered[0][:, 0:PACK, :])
+        weave(nc.vector.tensor_copy, dy_words[1][:, 0:P, :], gathered[1][:, 0:PACK, 0:P])
+        weave(nc.scalar.copy, dy_words[1][:, P:, :], gathered[1][:, 0:PACK, P:])
         dy_codes = keep.tile([P, N], U32, name="dy_codes", align_bytes=64)
         dy_scales = keep.tile([P, N], U8, name="dy_scales", align_bytes=64)
 
@@ -144,7 +158,7 @@ def tile_attend_gdelta_kernel(tc, dyT, oT, wo, gq, offs, out_0, out_1):
             nc.vector.tensor_tensor(do[j][:, lo:hi], bank[:], gate[:, lo:hi], MULT)
 
         quantize_dy(0)
-        wo_words = keep.tile([P, E * PACK], BF16, name="wo_words", tag="gathered0", align_bytes=64)
+        wo_words = keep.tile([P, E * PACK], BF16, name="wo_words", tag="gathered0", align_bytes=BURST)
         weave_wo(nc.vector.tensor_copy, 0, P // 2)
         weave_wo(nc.scalar.copy, P // 2, P)
         quantize_dy(1)
@@ -199,7 +213,7 @@ def tile_attend_gdelta_kernel(tc, dyT, oT, wo, gq, offs, out_0, out_1):
                 nc.scalar.activation(copied[:, c, :], sums[c][:], COPY, accum_out=delta_cols[:, c, 0:1])
             else:
                 nc.vector.tensor_reduce(delta_cols[:, c, 0:1], sums[c][:], AXIS_X, ADD)
-        delta_rows = keep.tile([P, BLOCKS, QUADRANT], F32, name="delta_rows", align_bytes=64)
+        delta_rows = keep.tile([P, BLOCKS, QUADRANT], F32, name="delta_rows", align_bytes=BURST)
         nc.vector.transpose(
             delta_rows[:].rearrange("p c k -> p (c k)"), delta_cols[:].rearrange("p c k -> p (c k)")
         )

@@ -28,7 +28,7 @@ HALF = N // 2
 RUN = T // P
 LINE = 4
 QUADRANT = 32
-SPLITS = (352, 320, 320)
+SPLITS = (352, 320, 352)
 BURST = 256
 
 
@@ -205,11 +205,12 @@ def tile_attend_gdelta_kernel(tc, dyT, oT, wo, gq, offs, out_0, out_1):
         for j in range(TILES - 1):
             add_to_delta(j, 0, N)
         add_to_delta(TILES - 1, 0, HALF)
-        add_to_delta(TILES - 1, HALF, N)
+        add_to_delta(TILES - 1, HALF, N - P)
+        add_to_delta(TILES - 1, N - P, N)
 
-        copied = keep.tile([P, 2, P], F32, name="copied")
+        copied = keep.tile([P, BLOCKS - 1, P], F32, name="copied")
         for c in range(BLOCKS):
-            if c < 2:
+            if c < BLOCKS - 1:
                 nc.scalar.activation(copied[:, c, :], sums[c][:], COPY, accum_out=delta_cols[:, c, 0:1])
             else:
                 nc.vector.tensor_reduce(delta_cols[:, c, 0:1], sums[c][:], AXIS_X, ADD)

from contextlib import ExitStack

import concourse.mybir as mybir
from concourse.masks import make_identity

D, E, T, N = 512, 512, 2048, 512
FLOPS = 2 * D * E * N
BYTES = 4 * (D * T + E * T + D * E + T + E * T + N) + 2 * 128 * (N // 16)

F32 = mybir.dt.float32
BF16 = mybir.dt.bfloat16
U32 = mybir.dt.uint32
U16 = mybir.dt.uint16
U8 = mybir.dt.uint8
E4M3 = mybir.dt.float8_e4m3fn_x4
E5M2 = mybir.dt.float8_e5m2_x4
MULT = mybir.AluOpType.mult
ADD = mybir.AluOpType.add
COPY = mybir.ActivationFunctionType.Copy
AXIS_X = mybir.AxisListType.X

P = 128
PACK = 4
BAND = 16
TILES = E // P
BLOCKS = N // P
HALF = N // 2
RUN = T // P
LINE = 4
QUADRANT = 32
SPLITS = (352, 320, 352)
BURST = 256


def tile_attend_gdelta_kernel(tc, dyT, oT, wo, gq, offs, out_0, out_1):
    nc = tc.nc
    with ExitStack() as ctx:
        keep = ctx.enter_context(tc.tile_pool(name="keep", bufs=1))
        psum = ctx.enter_context(tc.psum_pool(name="psum", bufs=1))

        offsets = keep.tile([P, N // BAND], U16, name="offsets", align_bytes=BURST)
        dy_first = keep.tile([P, T], F32, name="dy_first", align_bytes=BURST)
        dy_middle = keep.tile([P, 2 * T], F32, name="dy_middle", align_bytes=BURST)
        dy_last = keep.tile([P, T], F32, name="dy_last", align_bytes=BURST)
        o_tiles = [keep.tile([P, T], F32, name=f"o{j}", align_bytes=BURST) for j in range(TILES)]
        wo_raw = keep.tile([P, PACK, E], F32, name="wo_raw", align_bytes=BURST)
        dy_rows = dyT.rearrange("(p t) n -> p (t n)", t=PACK)

        gate_runs = keep.tile([P, RUN], F32, name="gate_runs", tag="gathered1", align_bytes=BURST)
        nc.scalar.dma_start(gate_runs[:], gq[0:1, :].rearrange("o (p u) -> (o p) u", u=RUN))
        nc.sync.dma_start(dy_first[:], dy_rows[:, 0:T])
        nc.sync.dma_start(offsets[:], offs)
        nc.sync.dma_start(dy_middle[:], dy_rows[:, T : 3 * T])
        nc.sync.dma_start(dy_last[:], dy_rows[:, 3 * T :])
        nc.sync.dma_start(wo_raw[:], wo.rearrange("(p t) c -> p t c", t=PACK))
        for j in range(TILES):
            nc.sync.dma_start(o_tiles[j][:], oT[j * P : (j + 1) * P, :])

        def listed(window, lo, hi):
            return window[:].indirect(offsets[:, lo // BAND : hi // BAND])

        windows = [keep.tile([P, T], F32, name=f"window{j}", align_bytes=BURST) for j in range(TILES)]
        nc.vector.memset(windows[0][:], 0.0)
        identity = keep.tile([P, P], F32, name="identity")
        make_identity(nc, identity[:])
        nc.vector.memset(windows[3][:], 0.0)
        delta_cols = keep.tile([P, BLOCKS, QUADRANT], F32, name="delta_cols", align_bytes=64)
        nc.gpsimd.memset(delta_cols[:], 0.0)
        zeros = keep.tile([P, N - min(SPLITS)], F32, name="zeros")
        nc.gpsimd.memset(zeros[:], 0.0)
        nc.gpsimd.memset(windows[1][:], 0.0)
        nc.gpsimd.memset(windows[2][:], 0.0)

        gate_window = keep.tile([P, T], F32, name="gate_window", tag="gathered0", align_bytes=BURST)
        for a in range(RUN // BLOCKS):
            spread = psum.tile([P, BLOCKS, P], F32, name=f"spread{a}", tag=f"bank{a}")
            for u in range(BLOCKS):
                column = a * BLOCKS + u
                nc.tensor.transpose(
                    spread[:, u, :], gate_runs[:, column : column + 1].to_broadcast([P, P]), identity[:]
                )
            nc.scalar.activation(
                gate_window[:].rearrange("p (k u) -> p k u", u=RUN)[:, :, a * BLOCKS : (a + 1) * BLOCKS],
                spread[:].rearrange("p u k -> p k u"),
                COPY,
            )
        gate = keep.tile([P, N], F32, name="gate", tag="gate")
        nc.vector.tensor_copy(gate[:], listed(gate_window, 0, N))

        gathered = [
            keep.tile([P, PACK + 2, HALF], BF16, name=f"gathered{h}", tag=f"gathered{h}", align_bytes=BURST)
            for h in range(2)
        ]
        dy_words = [
            keep.tile([P, HALF, PACK], BF16, name=f"dy_words{h}", tag=f"words{h}", align_bytes=64) for h in range(2)
        ]

        def gather_plane(t, window):
            nc.vector.tensor_copy(gathered[0][:, t, :], listed(window, 0, HALF))
            nc.scalar.activation(gathered[1][:, t, :], listed(window, HALF, N), COPY)

        gather_plane(0, dy_first)
        third = [rows[:, PACK:, :].rearrange("p a n -> p (a n)").bitcast(F32) for rows in gathered]
        nc.vector.tensor_copy(third[0], listed(dy_middle[:, T:], 0, HALF))
        nc.scalar.activation(third[1], listed(dy_middle[:, T:], HALF, N), COPY)
        gather_plane(1, dy_middle)
        nc.vector.tensor_copy(gathered[0][:, 2, :], third[0])
        nc.scalar.copy(gathered[1][:, 2, :], third[1])
        gather_plane(3, dy_last)

        def weave(copy, words, rows):
            copy(
                words.rearrange("p (c i) t -> p c t i", i=LINE),
                rows.rearrange("p t (c i) -> p c t i", i=LINE),
            )

        weave(nc.vector.tensor_copy, dy_words[0][:], gathered[0][:, 0:PACK, :])
        weave(nc.vector.tensor_copy, dy_words[1][:, 0:P, :], gathered[1][:, 0:PACK, 0:P])
        weave(nc.scalar.copy, dy_words[1][:, P:, :], gathered[1][:, 0:PACK, P:])
        dy_codes = keep.tile([P, N], U32, name="dy_codes", align_bytes=64)
        dy_scales = keep.tile([P, N], U8, name="dy_scales", align_bytes=64)

        def quantize_dy(h):
            nc.vector.quantize_mx(
                out=dy_codes[:, h * HALF : (h + 1) * HALF].bitcast(E5M2),
                scales=dy_scales[:, h * HALF : (h + 1) * HALF],
                in_=dy_words[h][:].rearrange("p n t -> p (n t)"),
            )

        wo_scales = keep.tile([P, E], U8, name="wo_scales", align_bytes=64)
        wo_codes = keep.tile([P, E], U32, name="wo_codes", align_bytes=64)
        stationary = [wo_codes[:, j * P : (j + 1) * P] for j in range(TILES)]

        def weave_wo(copy, lo, hi):
            words = wo_words[:, lo * PACK : hi * PACK].rearrange("p (c t) -> p c t", t=PACK)
            weave(copy, words, wo_raw[:, :, lo:hi])

        def quantize_wo(lo, hi):
            nc.vector.quantize_mx(
                out=wo_codes[:, lo:hi].bitcast(E4M3),
                scales=wo_scales[:, lo:hi],
                in_=wo_words[:, lo * PACK : hi * PACK],
            )

        do = [keep.tile([P, N], F32, name=f"do{j}") for j in range(TILES)]

        def gated_product(j, lo, hi, tag):
            bank = psum.tile([P, hi - lo], F32, name="product", tag=tag)
            nc.tensor.matmul_mx(
                out=bank[:],
                lhsT=stationary[j].bitcast(E4M3),
                lhsT_scale=wo_scales[:, j * P : (j + 1) * P],
                rhs=dy_codes[:, lo:hi].bitcast(E5M2),
                rhs_scale=dy_scales[:, lo:hi],
                start=True,
                stop=True,
            )
            nc.vector.tensor_tensor(do[j][:, lo:hi], bank[:], gate[:, lo:hi], MULT)

        quantize_dy(0)
        wo_words = keep.tile([P, E * PACK], BF16, name="wo_words", tag="gathered0", align_bytes=BURST)
        weave_wo(nc.vector.tensor_copy, 0, P // 2)
        weave_wo(nc.scalar.copy, P // 2, P)
        quantize_dy(1)
        quantize_wo(0, P)
        weave_wo(nc.vector.tensor_copy, P, 2 * P)
        weave_wo(nc.scalar.copy, 2 * P, E)
        quantize_wo(P, 2 * P)
        quantize_wo(2 * P, E)
        gated_product(0, 0, HALF, "bank0")
        gated_product(0, HALF, N, "product0")
        for j in range(1, TILES):
            gated_product(j, 0, N, f"product{j}")

        def store(j):
            nc.sync.dma_start(out_0[j * P : (j + 1) * P, :], windows[j][:])

        def scatter_on_scalar(j, lo, hi):
            nc.scalar.activation(listed(windows[j], lo, hi), do[j][:, lo:hi], COPY)

        scatter_on_scalar(0, 0, HALF)
        scatter_on_scalar(0, HALF, N)
        store(0)
        for j, split in enumerate(SPLITS, start=1):
            nc.vector.tensor_tensor(listed(windows[j], split, N), do[j][:, split:], zeros[:, 0 : N - split], ADD)
            scatter_on_scalar(j, 0, split)
            store(j)

        sums = [psum.tile([P, P], F32, name=f"sums{c}", tag=f"bank{c}") for c in range(BLOCKS)]
        products = keep.tile([P, TILES * N], F32, name="products", tag="gate")

        def add_to_delta(j, lo, hi):
            q = products[:, j * N + lo : j * N + hi]
            nc.vector.tensor_tensor(q, listed(o_tiles[j], lo, hi), do[j][:, lo:hi], MULT)
            for first in range(lo, hi, P):
                nc.tensor.matmul(
                    sums[first // P][:],
                    q[:, first - lo : first - lo + P],
                    identity[:],
                    start=(j == 0),
                    stop=(j == TILES - 1),
                    is_transpose=True,
                )

        for j in range(TILES - 1):
            add_to_delta(j, 0, N)
        add_to_delta(TILES - 1, 0, HALF)
        add_to_delta(TILES - 1, HALF, N - P)
        add_to_delta(TILES - 1, N - P, N)

        copied = keep.tile([P, BLOCKS - 1, P], F32, name="copied")
        for c in range(BLOCKS):
            if c < BLOCKS - 1:
                nc.scalar.activation(copied[:, c, :], sums[c][:], COPY, accum_out=delta_cols[:, c, 0:1])
            else:
                nc.vector.tensor_reduce(delta_cols[:, c, 0:1], sums[c][:], AXIS_X, ADD)
        delta_rows = keep.tile([P, BLOCKS, QUADRANT], F32, name="delta_rows", align_bytes=BURST)
        nc.vector.transpose(
            delta_rows[:].rearrange("p c k -> p (c k)"), delta_cols[:].rearrange("p c k -> p (c k)")
        )
        nc.scalar.dma_start(
            out_1.rearrange("o (c r k) -> (o r) c k", c=BLOCKS, k=QUADRANT),
            delta_rows[0:P:QUADRANT, :, :],
        )
